import numpy as np, ml_dtypes
CORES = [48,51,52,55]
N = 4
BF = ml_dtypes.bfloat16
L0, CAP, RO, B, OFF, H = 768, 128, 4, 384, (3, 1), 72
G = B * len(OFF); LM = L0 + RO * CAP; W0 = G + L0
Q0 = B // 2
def fit(x):
    return np.minimum(np.maximum(x, 0.0009765625), 2.0).astype(np.float32)
def places(lev, a):
    return np.concatenate([lev[(a + o) % N, :B] for o in OFF] + [lev[a]])
def body(rng, lev, lo, hi):
    gf = np.exp2(rng.uniform(-0.4, 0.4, (N, 8, 1, L0)))
    return fit((lev[:, None, None, :] * gf * rng.uniform(lo, hi, (N, 8, 16, L0))).reshape(N, 128, L0))
def weave(rng, lev, l, share):
    for a in range(N):
        key = np.log2(places(lev, a))
        for g in range(8):
            o = np.argsort(key + 0.4 * rng.standard_normal(W0)); at = np.argsort(o)[G:]
            near = o[np.clip(at + rng.integers(-48, 49, (16, L0)), 0, W0 - 1)]
            l[a, g] = np.where(rng.random(L0) < share, near, l[a, g])
    return l
def two(rng, n):
    i = rng.integers(0, 16, (8, 1, n)); return i, (i + rng.integers(1, 16, (8, 1, n))) % 16
def knife(rng, n):
    F = np.float32; h = F(0.5); q = F(0.75); z = rng.uniform(0.1, 0.6, (8192, 1)).astype(np.float32)
    x = (0.5 * np.reciprocal(1.0 - 0.75 * z.astype(np.float64))).astype(np.float32) + F(2.0 ** -24) * np.arange(-8, 9).astype(np.float32)
    say = ((x + h) - q * (z * x)) > 1; xs = []; zs = []
    for o in (((x + h) - (q * z) * x) > 1, ((x + h) - z * (q * x)) > 1, (x * (F(1) - q * z) + h) > 1, ((x - q * (z * x)) + h) > 1):
        i, j = np.nonzero(say != o); s = rng.integers(0, len(i), n)
        xs.append(x[i[s], j[s]]); zs.append(z[i[s], 0])
    return np.concatenate(xs), np.concatenate(zs)
def late(rng, x, l):
    alt = np.arange(16)[None, :, None] % 2; hub = 2 + np.arange(8)[:, None, None] // 3; D = 2 ** (RO - 1); f = 8 * RO
    x[:, :8] = 0.5 * (4 - RO); l[:, :, :8] = Q0 + alt * hub
    v = np.arange(8, f); rk = np.argsort(rng.random((128, len(v))), axis=0)
    x[:, v] = np.where(rk < H - 1, 1.5, np.where(rk == H - 1, 1.0 + 2.0 ** -24 * (v % 4) - 0.125 * (v // 8 + 1), 0.0)); l[:, :, v] = Q0 + alt
    o = rng.permutation(np.concatenate([np.arange(f, Q0), np.arange(Q0 + 5, L0)]))
    for s in range(RO - 2):
        c = o[s * CAP:(s + 1) * CAP]; rk = np.argsort(rng.random((128, CAP)), axis=0); n = rng.choice(np.array([H, H + 1, 128]), CAP)
        x[:, c] = np.where(rk < n, rng.uniform(1.001, 1.015, (128, CAP)) - 0.125 * (s + 1), 0.0); l[:, :, c] = Q0 + alt
    o = o[(RO - 2) * CAP:]
    for i in range(6):
        c = o[(D + 1) * i:(D + 1) * (i + 1)]; x[:, c] = 0.0; l[:, :, c[:D]] = G + c[1:]; l[:, :, c[D]] = Q0
        if i < 3:
            l[:, :, c[D - 1]] = G + Q0 + 2 + i; x[48 * i:48 * i + 48, c[0]] = 2.0
        else:
            b = rng.uniform(0.004, 0.03, 128).astype(np.float32); hit = (np.arange(16)[None, :] == rng.integers(0, 16, (8, 1))).reshape(-1); up = np.repeat((np.arange(8) + i) % 2 == 1, 16)
            x[:, c[0]] = b; x[:, c[D]] = np.where(hit & up, np.nextafter(b, np.float32(1)), np.where(hit, np.nextafter(b, np.float32(0)), b))
    o = o[6 * (D + 1):]; c = o[:24]; e = o[24:]
    x[:, c] = np.where(rng.random((128, 24)) < 0.1, 0.0009765625, 0.0); l[:, :, c] = G + c[rng.integers(0, 24, (8, 16, 24))]
    l[:, :, e] = G + e[rng.integers(0, len(e), (8, 16, len(e)))]
def pack(x, l):
    return {"x0": np.ascontiguousarray(x).astype(np.float32), "nb": np.ascontiguousarray(l.reshape(N, 128, L0)).astype(np.int32)}
def setup_inputs(rng):
    lev = np.exp2(rng.uniform(-3, 0.8, (N, L0)))
    return pack(body(rng, lev, 0.7, 1.3), weave(rng, lev, rng.integers(0, W0, (N, 8, 16, L0)), 0.4))
def setup_inputs_spread(rng):
    lev = np.exp2(rng.uniform(-9, 1, (N, L0))); l = np.minimum((W0 * rng.random((N, 8, 16, L0)) ** 3).astype(np.int64), W0 - 1)
    q = rng.permutation(N)[:N // 4]; lev[q] = np.exp2(rng.uniform(-9, -3, (len(q), L0)))
    s = rng.permutation(8)[:4]; l[:, s] = W0 - 1 - l[:, s]
    x = body(rng, lev, 0.25, 2.0); l = weave(rng, lev, l, 0.3)
    x[:, :, Q0:Q0 + 5] = 0.0; x[:, :, Q0 + 1] = 0.5; l[:, :, :, Q0:Q0 + 5] = Q0
    for j in range(3): x[:, 48 * j:48 * j + 48, Q0 + 2 + j] = 2.0
    for a in q: late(rng, x[a], l[a])
    return pack(x, l)
def setup_inputs_ends(rng):
    x = np.zeros((N, 128, L0)); l = np.zeros((N, 8, 16, L0), np.int64)
    for a in range(N):
        odd = a % 2; o = 1 + rng.permutation(L0 - 2); n = CAP - 2 if odd else CAP + 1 + int(rng.integers(0, L0 // 8))
        c = rng.choice(np.array([0, H - 1, H - 1]), L0); c[o[:n]] = rng.choice(np.array([H, H, 128]), n)
        c[0] = 128 * odd; c[L0 - 1] = 128 * odd
        x[a] = 2.0 * (np.argsort(rng.random((128, L0)), axis=0) < c)
        e = np.where(rng.random((8, 16, L0)) < 0.5, 0, W0 - 1)
        k = np.where(rng.random((8, 16, L0)) < 0.72, e, rng.integers(0, W0, (8, 16, L0)))
        i, j = two(rng, L0); np.put_along_axis(k, i, 0, 1); np.put_along_axis(k, j, W0 - 1, 1)
        same = (rng.random((8, 1, L0)) < 0.15) & (c < H)
        l[a] = np.where(same, e[:, :1], k)
    return pack(x, l)
def setup_inputs_corners(rng):
    nc = L0 // 8; x = np.zeros((N, 128, L0)); l = rng.integers(0, W0, (N, 8, 16, L0)); me = G + np.arange(L0)
    want = np.array([CAP, CAP + 1, L0 - nc, CAP - 1, 0, 1, CAP, L0 - nc])[:N][rng.permutation(N)]
    for a in range(N):
        o = rng.permutation(L0)
        if want[a] == L0 - nc: o = np.concatenate([o[o >= 256], o[o < 256]])
        cold = o[:nc]; hot = o[nc:nc + int(want[a])]
        c = rng.choice(np.array([0, 1, H - 1, H - 1]), L0); c[hot] = rng.choice(np.array([H, H, H + 1, 127, 128]), len(hot))
        hi = np.where(rng.random((128, L0)) < 0.25, 2.0, rng.uniform(1.5, 2.0, (128, L0)))
        lo = np.where(rng.random((128, L0)) < 0.25, 0.5, rng.uniform(0.0625, 0.5, (128, L0)))
        x[a] = np.where(np.argsort(rng.random((128, L0)), axis=0) < c, hi, lo)
        x[a][:, cold] = rng.uniform(0.015625, 0.03125, (128, nc))
        kd = rng.permutation(8)
        l[a, kd[1]] = me
        l[a, kd[2]] = rng.choice(np.array([G, G + L0 - 1]), (16, L0))
        l[a, kd[3]] = rng.choice(np.array([0, G - 1]), (16, L0))
        l[a, kd[4]] = rng.integers(0, W0, L0)
        l[a, kd[5]] = np.maximum(me - 1, G)
        l[a, kd[6]] = G + (np.arange(L0) ^ 1)
        l[a, kd[7]] = int(rng.integers(0, W0))
        i, j = two(rng, L0); np.put_along_axis(l[a], i, G + cold[rng.integers(0, nc, (8, 1, L0))], 1)
        l[a][:, :, cold] = G + cold[rng.integers(0, nc, (8, 16, nc))]
    return pack(x, l)
def setup_inputs_close(rng):
    nq = L0 // 8; nf = 24; base = rng.uniform(0.25, 1.9, (nf, 128)).astype(np.float32); fam = rng.integers(0, nf, (N, L0))
    base[:, 96:] = base[:, 96:] * np.float32(0.03125)
    v = np.ascontiguousarray(base[fam].transpose(0, 2, 1)).reshape(N, 8, 16, L0)
    hit = np.arange(16)[None, None, :, None] == rng.integers(0, 16, (N, 8, 1, L0)); kind = rng.integers(0, 3, (N, 8, 1, L0))
    v = np.where(hit & (kind == 1), np.nextafter(v, np.float32(4)), np.where(hit & (kind == 2), np.nextafter(v, np.float32(0)), v))
    x = np.ascontiguousarray(v).reshape(N, 128, L0); l = rng.integers(0, W0, (N, 8, 16, L0)); unit = 2.0 ** -24
    for a in range(N):
        pf = places(fam, a); o = np.argsort(pf, kind="stable"); first = np.searchsorted(pf[o], np.arange(nf)); cnt = np.bincount(pf, minlength=nf)
        mates = o[first[fam[a]] + (rng.random((8, 16, L0)) * cnt[fam[a]]).astype(np.int64)]
        l[a] = np.where(rng.random((8, 16, L0)) < 0.75, mates, l[a])
        rk = np.argsort(rng.random((128, nq)), axis=0)
        x[a, :, :nq] = np.where(rk < H - 1, 1.5, np.where(rk == H - 1, 0.5 + unit * rng.integers(0, 4, nq), np.where(rk < H + 3, 0.5 + unit * rng.integers(0, 2, (128, nq)), 0.25)))
        x[a, :, nq:nq + 8] = 2.0; x[a, :, nq + 8:nq + 16] = 0.0
        i, j = two(rng, nq); k = l[a][:, :, :nq].copy()
        np.put_along_axis(k, i, G + nq + rng.integers(0, 8, (8, 1, nq)), 1); np.put_along_axis(k, j, G + nq + 8 + rng.integers(0, 8, (8, 1, nq)), 1)
        l[a][:, :, :nq] = k
        c = nq + 16 + np.arange(48); xe, ze = knife(rng, 12); rk = np.argsort(rng.random((128, 48)), axis=0)
        x[a][:, c] = np.where(rk < H - 1, 1.5, np.where(rk == H - 1, xe, 0.25))
        x[a][:, c + 48] = np.where(rk == H - 1, ze, rng.uniform(0.1, 0.6, (128, 48)))
        i, j = two(rng, 48); k = np.where(rng.random((8, 16, 48)) < 0.5, G + nq + rng.integers(0, 8, (8, 16, 48)), G + c + 48)
        np.put_along_axis(k, i, G + nq + rng.integers(0, 8, (8, 1, 48)), 1); np.put_along_axis(k, j, G + c[None, None, :] + 48, 1)
        l[a][:, :, c] = k
    return pack(x, l)
def setup_inputs_calm(rng):
    lev = rng.uniform(0.1, 0.35, (N, L0)); x = lev[:, None, :] * rng.uniform(0.9, 1.1, (N, 128, L0)); n = rng.permutation(N) % 4
    for a in range(N):
        x[a][:, rng.permutation(L0)[:int(n[a])]] = 2.0
    return pack(x, rng.integers(0, W0, (N, 8, 16, L0)))
def check_inputs(d):
    bad = []; x = np.asarray(d["x0"]).astype(np.float64)
    if not (np.min(x) >= 0 and np.max(x) <= 2): bad.append("range of x0")
    if np.any((x > 0) & (x < 0.0009765625)): bad.append("small numbers of x0")
    if np.min(d["nb"]) < 0 or np.max(d["nb"]) > W0 - 1: bad.append("range of nb")
    return bad
def reference(x0, nb):
    F = np.float32
    x = np.zeros((N, 128, LM), np.float32); x[:, :, :L0] = x0
    l = np.zeros((N, 8, 16, LM), np.int64); l[:, :, :, :L0] = nb.reshape(N, 8, 16, L0)
    live = [L0] * N
    for t in range(RO):
        old = np.array(x)
        for a in range(N):
            n = live[a]; own = old[a, :, :n]
            w = np.concatenate([old[(a + o) % N, :, :B] for o in OFF] + [own], axis=1)
            xn = np.zeros((128, n), np.float32); mv = np.zeros((8, 16, n), np.int64)
            for g in range(8):
                c = own[16 * g:16 * g + 16]; k = np.array(l[a, g, :, :n])
                p = np.take(w[16 * g:16 * g + 16], k, axis=1)
                y = np.maximum.reduce(p, axis=1); z = np.minimum.reduce(p, axis=1)
                xn[16 * g:16 * g + 16] = np.minimum(np.maximum((c + F(0.25) * y) - F(0.75) * (z * c), F(0)), F(2))
                none = np.logical_not(np.any(p > c[:, None, :], axis=0))
                mv[g] = np.where(none & (k >= G), np.take_along_axis(k, np.maximum(k - G, 0), 1), k)
            ready = (np.add.reduce((xn > 1).astype(np.int64), axis=0) >= H).astype(np.int64)
            m = np.flatnonzero((ready == 1) & (np.add.accumulate(ready) <= CAP)); ch = n + np.arange(len(m))
            xn[:, m] = xn[:, m] * F(0.5)
            x[a, :, :n] = xn; x[a][:, ch] = xn[:, m]
            l[a, :, :, :n] = mv; l[a][:, :, ch] = mv[:, :, m]
            l[a][:, t, ch] = G + m; l[a][:, t, m] = G + ch
            live[a] = n + len(m)
    return {"yx": x, "yn": l.reshape(N, 128, LM).astype(np.float32)}

@@ -1,0 +1,664 @@
+from concourse.bass import DstId, RemoteDMATransfer
+from concourse.mybir import AluOpType, ActivationFunctionType
+
+N = 4
+L0, CAP, RO, B, OFF, H = 768, 128, 4, 384, (3, 1), 72
+G = B * len(OFF)
+LM = L0 + RO * CAP
+NP = G + LM
+VOID = NP - 1
+LP = 32
+BIG = 4096.0
+
+CFG = {
+    "KD": 10,
+    "KV": [[6, 0, 0], [3, 0, 0], [3, 0, 0], [3, 0, 0]],
+    "AS": "yz",
+    "look": 0.0,
+    "KC": 4,
+    "VU": {t: [(0, "z"), (1, "z"), (2, "z")] for t in range(4)},
+    "f": 1.2, "gath": 1.5, "scat": 3.8, "bw": 280.0, "fix": 40.0, "sem": 70.0, "rlat": 2200.0, "riss": 600.0,
+    "dlat": 1800.0, "diss": 120.0, "first": 2500.0,
+}
+
+INST = [(t, c) for t in range(RO) for c in range(3) if (c < 2 or t > 0)]
+
+
+def width(t, c):
+    return B if c < 2 else CAP * t
+
+
+SCRATCH = {
+    "X0": ("sbuf", [128, NP], "float32"), "X1": ("sbuf", [128, NP], "float32"),
+    "W0": ("sbuf", [128, NP], "float32"), "W1": ("sbuf", [128, NP], "float32"),
+    "L": ("sbuf", [128, LM + 2 * LP], "float32"),
+    "NB": ("sbuf", [128, L0], "int32"),
+    "P0": ("sbuf", [128, 16 * B], "float32"), "P1": ("sbuf", [128, 16 * B], "float32"), "P2": ("sbuf", [128, 16 * B], "float32"),
+    "Q0": ("sbuf", [128, 16 * B], "float32"), "Q1": ("sbuf", [128, 16 * B], "float32"),
+    "C0": ("sbuf", [128, 16 * B], "bfloat16"), "C1": ("sbuf", [128, 16 * B], "bfloat16"),
+    "QD": ("sbuf", [128, 3 * B], "float32"),
+    "YZ": ("sbuf", [128, 6 * B], "float32"),
+    "TR0": ("sbuf", [128, 2 * B + 32], "float32"), "TR1": ("sbuf", [128, 2 * B + 32], "float32"),
+    "OT": ("sbuf", [128, 3 * B], "uint16"),
+    "BV": ("sbuf", [128, 3 * B], "bfloat16"),
+    "T1": ("sbuf", [128, B], "float32"), "T3": ("sbuf", [128, 3 * B], "float32"), "T5": ("sbuf", [128, B], "float32"),
+    "PL": ("sbuf", [128, LM], "float32"),
+    "IM": ("sbuf", [128, 144], "float32"), "I2": ("sbuf", [128, 24], "float32"), "I16": ("sbuf", [128, 128], "float32"),
+    "PI": ("sbuf", [128, 8], "int32"), "CF": ("sbuf", [128, 16], "float32"), "NM": ("sbuf", [128, 16], "float32"),
+    "LS": ("sbuf", [128, 48], "uint16"),
+    "YB": ("sbuf", [128, 144], "bfloat16"), "ID": ("sbuf", [128, 128], "float32"), "NI": ("sbuf", [128, 128], "float32"),
+    "ND": ("sbuf", [128, 128 * max(1, 16 - CFG["KD"])], "float32"),
+    "TRI": ("sbuf", [128, 128], "bfloat16"), "ONE": ("sbuf", [128, 128], "bfloat16"), "E1": ("sbuf", [128, 128], "bfloat16"),
+    "BM": ("sbuf", [128, 128], "float32"), "MA": ("sbuf", [128, 8], "float32"), "WE": ("sbuf", [128, 8], "float32"),
+    "RR": ("sbuf", [128, 18], "bfloat16"),
+    "RB": ("sbuf", [128, 16], "bfloat16"), "RS": ("sbuf", [128, 16], "bfloat16"), "CR": ("sbuf", [128, 16], "float32"),
+    "HH": ("sbuf", [128, 9 * 128], "bfloat16"),
+    "ST": ("sbuf", [128, 32], "float32"), "RW": ("sbuf", [128, 8], "float32"),
+    "MO": ("sbuf", [128, 8], "uint16"), "CO": ("sbuf", [128, 8], "uint16"),
+    "KK": ("sbuf", [128, 128], "float32"), "CH": ("sbuf", [128, 128], "float32"), "FF": ("sbuf", [128, 128], "float32"),
+    "GG": ("sbuf", [128, 128], "float32"), "XM": ("sbuf", [128, 128], "float32"), "LA": ("sbuf", [128, 128], "float32"),
+    "LC": ("sbuf", [128, 128], "float32"),
+    "XP0": ("psum", [128, 512], "float32"), "XP1": ("psum", [128, 512], "float32"), "XP2": ("psum", [128, 512], "float32"),
+    "VL0": ("psum", [128, 512], "float32"), "VL1": ("psum", [128, 512], "float32"), "VL2": ("psum", [128, 512], "float32"),
+    "S0": ("psum", [128, 512], "float32"), "S1": ("psum", [128, 512], "float32"),
+}
+
+SEMAPHORES = (["eV", "eA", "eP", "eG", "hback"] + ["ld%d" % i for i in range(4)] + ["st%d" % i for i in range(4)] + ["wt%d" % i for i in range(RO - 1)]
+              + ["gl%d" % i for i in range(RO)] + ["ga%d" % i for i in range(RO)] + ["gb%d" % i for i in range(RO)]
+              + ["%s%d" % (s, i) for s in ("fl", "ha", "ya", "dq") for i in range(len(INST))])
+
+ESEM = {"V": "eV", "A": "eA", "P": "eP", "G": "eG"}
+Op = AluOpType
+Fn = ActivationFunctionType
+
+
+def helper_of(core, T, topo):
+    mates = [c for c in topo.cores_of(core) if topo.die(c) == topo.die(core)]
+    ranks = [c for c in mates if T.rank_of(c) is not None]
+    free = [c for c in mates if T.rank_of(c) is None]
+    return free[ranks.index(core) % len(free)]
+
+
+def fold_units(t, c):
+    return [u for u in ("y", "z") if (c, u) not in CFG["VU"].get(t, [])]
+
+
+def fold_cols(t, c):
+    w = width(t, c)
+    us = fold_units(t, c)
+    lo = 2 * B * c + (0 if "y" in us else w)
+    return lo, lo + w * len(us)
+
+
+def mask_of(engines):
+    m = 0
+    for e in engines:
+        m |= 1 << e
+    return m
+
+
+def build():
+    ops = []
+    hist = {}
+    bysem = {}
+    late = []
+    cyc = 0.83 * CFG["f"]
+    KD, KC = CFG["KD"], CFG["KC"]
+
+    def psum(name):
+        return name in SCRATCH and SCRATCH[name][0] == "psum"
+
+    def regs(a):
+        if a[0] == "ind":
+            return [a[1], a[2]]
+        return [a]
+
+    def add(eng, kind, args, reads, writes, cost, group=None, after=(), **kw):
+        o = dict(id=len(ops), eng=eng, kind=kind, args=args, cost=cost, group=group, deps=set(after), **kw)
+        acc = [(r, False) for r in reads] + [(r, True) for r in writes]
+        for r, wr in acc:
+            for (lo, hi, oid, ow, oe, og) in hist.get(r[0], []):
+                if group is not None and og == group and wr and ow:
+                    continue
+                if psum(r[0]) and oe != eng:
+                    o["deps"].add(oid)
+                elif (wr or ow) and lo < r[2] and r[1] < hi:
+                    o["deps"].add(oid)
+        for d in list(o["deps"]):
+            if "sem" in ops[d]:
+                o["deps"].update(bysem[ops[d]["sem"]])
+        if "sem" in o:
+            bysem.setdefault(o["sem"], []).append(o["id"])
+        for r, wr in acc:
+            h = hist.setdefault(r[0], [])
+            if wr and group is None and len(r) == 3 and not psum(r[0]) and not kw.get("part"):
+                h[:] = [x for x in h if not (r[1] <= x[0] and x[1] <= r[2])]
+            h.append((r[1], r[2], o["id"], wr, eng, group))
+        ops.append(o)
+        return o["id"]
+
+    def nel(a):
+        if a[0] == "ind":
+            return 16 * (a[2][2] - a[2][1])
+        return len(range(a[1], a[2], a[3] if len(a) > 3 else 1))
+
+    def two(a):
+        return SCRATCH[a[0]][2] in ("bfloat16", "uint16")
+
+    def comp(eng, kind, out, ins, args, mult=1.0):
+        reads, writes = [], []
+        for a in ins:
+            if isinstance(a, tuple):
+                reads += regs(a)
+        part = False
+        if out[0] == "ind":
+            writes.append(out[1]); reads.append(out[2]); part = True
+            cost = 50 + nel(out) * CFG["scat"] * cyc
+        else:
+            writes.append(out)
+            if isinstance(ins[0], tuple) and ins[0][0] == "ind":
+                cost = (50 if eng == "V" else 65) + nel(out) * CFG["gath"] * cyc
+            else:
+                cost = CFG["fix"] + max(64, nel(out) * mult) * cyc
+        return add(eng, kind, (out, ins, args), reads, writes, cost, part=part)
+
+    def ts(out, a, s1, op0, s2=None, op1=None):
+        half = a[0] != "ind" and out[0] != "ind" and two(a) and two(out)
+        return comp("V", "ts", out, [a, s1, s2], (op0, op1), 0.5 if half else 1.0)
+
+    def tt(out, a, b, op):
+        both = a[0] != "ind" and not psum(a[0]) and not psum(b[0])
+        return comp("V", "tt", out, [a, b], op, 2.0 if both else 1.0)
+
+    def cp(out, a):
+        return comp("V", "cp", out, [a], None)
+
+    def act(out, a, fn, scale=None):
+        return comp("A", "act", out, [a], (fn, scale))
+
+    def mm(out, lhs, rhs, group=None):
+        k = 4 if SCRATCH[rhs[0]][2] == "float32" else 1
+        return add("P", "mm", (out, lhs, rhs), [lhs, rhs], [out], 15 + max(64, nel(rhs)) * k * cyc / 2, group=group)
+
+    def iota(out, pattern, base, cm=0):
+        return add("G", "iota", (out, pattern, base, cm), [], [out], 130 + 2 * nel(out) * cyc, soft=list(late))
+
+    def fill(out, val):
+        return iota(out, [[0, nel(out)]], val)
+
+    def dma(eng, out, a, sem, nbytes, group=None, rows=None):
+        return add(eng, "dma", (out, a, rows), [a], [out], CFG["diss"], group=group, sem=sem, inc=16, nbytes=nbytes, lat=CFG["dlat"],
+                   part=rows is not None)
+
+    def send(t, buf):
+        s = add("G", "send", (buf, t), [(buf, G, G + B)], [], CFG["riss"], sem="gl%d" % t, inc=16, nbytes=2 * 128 * B * 4, lat=CFG["rlat"])
+        if t == 0:
+            late.append(s)
+        for d in range(2):
+            add("X", "arrive", None, [], [(buf, d * B, d * B + B)], 300.0, after=[s], sem=("ga%d", "gb%d")[d] % t, inc=8)
+
+    def col(name, j):
+        return (name, j, j + 1)
+
+    E = ("IM", 15, 143)
+
+    def esl(n):
+        return ("IM", 15, 15 + n)
+
+    cP, cB, cG, cPB, cE, cHB, cDF, cC1, cD8, cD24, cND = [col("CF", j) for j in range(11)]
+
+    dma("S", ("X0", G, G + B), ("x0", 0, B), "ld0", 128 * B * 4)
+    dma("A", ("NB", 0, B), ("nb", 0, B), "ld1", 128 * B * 4)
+    dma("A", ("NB", B, L0), ("nb", B, L0), "ld2", 128 * B * 4)
+    dma("S", ("X0", G + B, G + L0), ("x0", B, L0), "ld3", 128 * B * 4)
+    iota(("PI", 0, 1), [[0, 1]], 0, 1)
+    iota(("IM", 0, 144), [[1, 144]], -15)
+    iota(("I2", 0, 24), [[256, 3], [2, 8]], 0)
+    fill(("L", 0, LP), 0)
+    fill(("L", LP + L0, LP + L0 + LP), VOID)
+    send(0, "X0")
+    late.append(iota(("W0", 0, G), [[1, G]], 0))
+    fill(("L", LP + L0 + LP, LP + LM - CAP), VOID)
+    fill(("L", LP + LM - CAP, LM + 2 * LP), 0)
+    fill(("W0", G + L0, NP), VOID)
+    fill(("X0", G + L0, NP), 0)
+    fill(("QD", 0, 3 * B), 0)
+    fill(("X1", G + L0, NP), 0)
+    iota(("I16", 0, 128), [[0, 8], [1, 16]], 0)
+    fill(("ONE", 0, 128), 1)
+    fill(("RB", 0, 16), 0)
+    fill(("RS", 0, 16), 0)
+    fill(("ST", 0, 1), L0)
+    iota(("PL", 0, LM), [[1, LM]], G)
+    iota(("W1", 0, G), [[1, G]], 0)
+    fill(("W1", G + L0, NP), VOID)
+    p0 = col("PI", 0)
+    ts(col("PI", 1), p0, 15, Op.bitwise_and)
+    ts(col("PI", 2), p0, 112, Op.bitwise_and)
+    ts(col("PI", 3), p0, 1, Op.bitwise_and)
+    ts(col("PI", 4), p0, 4, Op.logical_shift_right, 1, Op.bitwise_and)
+    ts(col("PI", 5), p0, 3, Op.logical_shift_right, 1, Op.bitwise_and)
+    cp(("CF", 0, 6), ("PI", 0, 6))
+    ts(cDF, cPB, cE, Op.not_equal, float(B + 16), Op.mult)
+    ts(cC1, cB, 16.0, Op.mult, cDF, Op.add)
+    ts(cD24, cHB, float(1 - B), Op.mult, cC1, Op.add)
+    ts(("LS", 0, 24, 3), ("I2", 0, 8), cC1, Op.add)
+    ts(("LS", 1, 24, 3), ("I2", 8, 16), cD24, Op.add)
+    ts(("LS", 2, 24, 3), ("I2", 16, 24), cC1, Op.add, float(1 - B), Op.add)
+    ts(cD8, cHB, -127.0, Op.mult, cC1, Op.add)
+    ts(("LS", 24, 32), ("I2", 0, 8), cD8, Op.add)
+    ts(("LS", 32, 48), esl(16), cC1, Op.add)
+    lists = {B: ("LS", 0, 24), 128: ("LS", 24, 32), 256: ("LS", 32, 48)}
+    ts(("ID", 0, 128), E, cP, Op.is_equal)
+    ts(("YB", 0, 144), ("IM", 0, 144), cG, Op.is_equal, BIG, Op.mult)
+    ts(("NM", 0, 16), esl(16), cB, Op.is_equal, -1.0, Op.mult)
+    for k in range(KD, 16):
+        ts(("ND", 128 * (k - KD), 128 * (k - KD + 1)), E, cP, Op.is_equal, col("NM", k), Op.mult)
+    if KD:
+        ts(cND, cB, float(KD), Op.is_lt, -1.0, Op.mult)
+        ts(("NI", 0, 128), E, cP, Op.is_equal, cND, Op.mult)
+    ts(("TRI", 0, 128), E, cP, Op.is_ge)
+    ts(("E1", 0, 128), E, 1.0, Op.add)
+    ts(("BM", 0, 128), ("I16", 0, 128), cB, Op.is_equal)
+    ts(("MA", 0, 8), esl(8), 16.0, Op.mult, cG, Op.is_equal)
+    ts(("WE", 0, 8), esl(8), 16.0, Op.mult, cB, Op.add)
+    ts(("RR", 0, 18, 2), esl(9), 0.0, Op.mult, cP, Op.add)
+    ts(("RR", 1, 18, 2), esl(9), 128.0, Op.mult)
+    for c in range(2):
+        cp(("L", LP + B * c, LP + B * c + B), ("NB", B * c, B * c + B))
+        act(("W0", G + B * c, G + B * c + B), ("L", LP + B * c, LP + B * c + B), Fn.Copy)
+
+    ntr = [0]
+    prevq = []
+
+    def offsets(c, w):
+        tr = "TR%d" % (ntr[0] % 2)
+        ntr[0] += 1
+        c0 = LP + B * c
+        comp("V", "tr", (tr, 0, w), [("L", c0, c0 + w)], None)
+        comp("V", "tr", (tr, B, B + w + 32), [("L", c0 - 16, c0 + w + 16)], None)
+        cp(("OT", B * c, B * c + w), ("ind", (tr, 0, B + w + 32), lists[w]))
+
+    def xcopy(buf, c, w):
+        mm(("XP%d" % c, 0, w), ("ID", 0, 128), (buf, G + B * c, G + B * c + w))
+
+    def kcalls(lo, hi):
+        n = hi - lo
+        if n <= 0:
+            return []
+        m = (n + KC - 1) // KC
+        cuts = [lo + (n * i) // m for i in range(m + 1)]
+        return list(zip(cuts[:-1], cuts[1:]))
+
+    for c in range(2):
+        offsets(c, B)
+        xcopy("X0", c, B)
+
+    for t in range(RO):
+        X, XN, W, WN = "X%d" % (t % 2), "X%d" % (1 - t % 2), "W%d" % (t % 2), "W%d" % (1 - t % 2)
+        chunks = [c for c in range(3) if width(t, c)]
+        nb = (L0 + CAP * t) // 128
+        cN, cNN = col("ST", t), col("ST", t + 1)
+        cNPE, cTR, cINV, cMM = [col("ST", 8 + j) for j in range(4)]
+        last = t == RO - 1
+        top = NP if t else G + L0
+        if last:
+            fill((W, VOID, NP), 0)
+        ts(cNPE, cN, cP, Op.add)
+        if t:
+            ts(("CO", 0, 8), ("WE", 0, 8), cN, Op.add, float(-L0), Op.add)
+        ts(("CH", 0, 128), E, cN, Op.add, float(G), Op.add)
+        for c in chunks:
+            i = INST.index((t, c))
+            w = width(t, c)
+            A = w // 16
+            Pb, Cb, XP = "P%d" % c, "C%d" % (i % 2), ("XP%d" % c, 0, w)
+            o0 = B * c
+
+            def sl(buf, k0, k1=None):
+                return (buf, k0 * w, (k0 + 1 if k1 is None else k1) * w)
+
+            KV = CFG["KV"][t][c]
+            for k0, k1 in kcalls(0, KV):
+                cp(sl(Pb, k0, k1), ("ind", (X, 0, top), ("OT", o0 + k0 * A, o0 + k1 * A)))
+            for k0, k1 in kcalls(KV, 16):
+                act(sl(Pb, k0, k1), ("ind", (X, 0, top), ("OT", o0 + k0 * A, o0 + k1 * A)), Fn.Copy)
+            us = fold_units(t, c)
+            if us:
+                lo, hi = fold_cols(t, c)
+                f = add("G", "fold", (i, t, c), [(Pb, 0, 16 * w)], [("YZ", lo, hi)], CFG["riss"], sem="fl%d" % i, inc=16,
+                        nbytes=len(us) * 16 * 128 * w * 4, lat=CFG["rlat"])
+                add("X", "arrive", None, [], [("YZ", lo, hi)], CFG["riss"] + CFG["rlat"] + 128 * (hi - lo) * 4 / CFG["bw"] + 300, after=[f],
+                    sem="ya%d" % i, inc=16)
+            for k in range(16):
+                tt(sl(Cb, k), sl(Pb, k), XP, Op.is_gt)
+                mm(("VL%d" % c, 0, w), ("YB", 15 - k, 143 - k), sl(Cb, k), group=("vl", i))
+            T3 = T4 = ("T3", o0, o0 + w)
+            T1, T2, T5, S0 = ("T1", 0, w), ("S1", 0, w), ("T5", 0, w), ("S0", 0, w)
+            for u in ("z", "y"):
+                if u in us:
+                    src = ("YZ", 2 * o0, 2 * o0 + w) if u == "y" else ("YZ", 2 * o0 + w, 2 * o0 + 2 * w)
+                else:
+                    op = Op.max if u == "y" else Op.min
+                    tt(S0, sl(Pb, 0), sl(Pb, 1), op)
+                    for k in range(2, 16):
+                        tt(S0, sl(Pb, k), S0, op)
+                    src = S0
+                if u == "z":
+                    tt(T3, src, XP if u in us else (X, G + o0, G + o0 + w), Op.mult)
+                    if "z" in CFG["AS"] and c != chunks[-1]:
+                        act(T4, T3, Fn.Copy, 0.75)
+                    else:
+                        ts(T4, T3, 0.75, Op.mult)
+                elif "y" in CFG["AS"] and u in us and c != chunks[-1]:
+                    act(T1, src, Fn.Copy, 0.25)
+                else:
+                    ts(T1, src, 0.25, Op.mult)
+            tt(T2, T1, XP, Op.add)
+            tt(T5, T2, T4, Op.subtract)
+            ts(("BV", o0, o0 + w), T5, 1.0, Op.is_gt)
+            ts((XN, G + o0, G + o0 + w), T5, 0.0, Op.max, 2.0, Op.min)
+            for j in range(o0 // 128, (o0 + w) // 128):
+                mm(col("S1", B + j), ("BV", 128 * j, 128 * j + 128), ("ONE", 0, 1))
+        for c in chunks:
+            i = INST.index((t, c))
+            w = width(t, c)
+            A = w // 16
+            Qb = "Q%d" % (i % 2)
+            o0 = B * c
+            for k0, k1 in kcalls(KD, 16) + kcalls(0, KD):
+                j = act((Qb, k0 * w, k1 * w), ("ind", (W, 0, top), ("OT", o0 + k0 * A, o0 + k1 * A)), Fn.Abs)
+                ops[j]["soft"] = prevq[-1:]
+                prevq.append(j)
+            for k in range(KD):
+                dma("S", ("QD", o0, o0 + w), (Qb, k * w, k * w + w), "dq%d" % i, 8 * w * 4, group=("dq", i), rows=k)
+            for k in range(KD, 16):
+                mm(("VL%d" % c, 0, w), ("ND", 128 * (k - KD), 128 * (k - KD + 1)), (Qb, k * w, k * w + w), group=("vl", i))
+            if KD:
+                mm(("VL%d" % c, 0, w), ("NI", 0, 128), ("QD", o0, o0 + w), group=("vl", i))
+        c0, c1, c2, c3 = B, B + 16, B + 32, B + 48
+        ts(("RB", 0, nb), ("S1", c0, c0 + nb), float(H), Op.is_ge)
+        comp("V", "scan", ("RS", 1, nb + 1), [("ONE", 0, nb), ("RB", 0, nb)], None)
+        mm(("S1", c1, c1 + nb + 1), ("TRI", 0, 128), ("RB", 0, nb + 1), group=("c", t))
+        mm(("S1", c1, c1 + nb + 1), ("ONE", 0, 128), ("RS", 0, nb + 1), group=("c", t))
+        tot = col("S1", c1 + nb)
+        tt(("CR", 0, nb), ("S1", c1, c1 + nb), ("RB", 0, nb), Op.mult)
+        ts(cINV, cP, tot, Op.is_ge, cNPE, Op.mult)
+        ts(cTR, tot, col("NM", t), Op.mult, -1.0, Op.mult)
+        if not last:
+            ts(cNN, tot, float(CAP), Op.min, cN, Op.add)
+        for j in range(nb):
+            ts(("HH", 128 * j, 128 * j + 128), ("E1", 0, 128), col("CR", j), Op.is_equal)
+        for j in range(nb):
+            mm(("S1", c2, c2 + 2), ("HH", 128 * j, 128 * j + 128), ("RR", 2 * j, 2 * j + 2), group=("m", t))
+        ts(("KK", 0, 128), E, cTR, Op.is_ge, 2 * BIG, Op.mult)
+        tt(("FF", 0, 128), ("KK", 0, 128), ("CH", 0, 128), Op.subtract)
+        ts(cMM, col("S1", c2), col("S1", c2 + 1), Op.add, cINV, Op.add)
+        ts(("RW", 0, 8), ("MA", 0, 8), cMM, Op.mult)
+        mm(("S1", c3, c3 + 8), ("BM", 0, 128), ("RW", 0, 8))
+        MO, CO = ("MO", 0, 8), ("CO", 0, 8)
+        cp(MO, ("S1", c3, c3 + 8))
+        XM = ("XM", 0, 128)
+        ts(XM, ("ind", (XN, G, NP), MO), 0.5, Op.mult)
+        cp(("ind", (XN, G, NP), MO), XM)
+        if not last:
+            send(t + 1, XN)
+            for c in range(2):
+                xcopy(XN, c, B)
+        else:
+            dma("S", ("yx", 0, L0), (XN, G, G + L0), "st0", 128 * L0 * 4)
+        if t:
+            cp(("ind", (XN, G + L0, NP), CO), XM)
+        else:
+            cp((XN, G + L0, G + L0 + CAP), XM)
+        if not last:
+            xcopy(XN, 2, width(t + 1, 2))
+        else:
+            dma("S", ("yx", L0, LM), (XN, G + L0, NP), "st1", 128 * (LM - L0) * 4)
+        Lw = ("L", LP, LP + LM)
+        tt(("LA", 0, 128), ("ind", Lw, MO), ("FF", 0, 128), Op.min)
+        cp(("ind", Lw, MO), ("LA", 0, 128))
+        tt(("GG", 0, 128), ("ind", ("PL", 0, LM), MO), ("KK", 0, 128), Op.add)
+        for c in chunks:
+            w = width(t, c)
+            o0 = B * c
+            tt((WN, G + o0, G + o0 + w), ("L", LP + o0, LP + o0 + w), ("VL%d" % c, 0, w), Op.min)
+            act(("L", LP + o0, LP + o0 + w), (WN, G + o0, G + o0 + w), Fn.Abs)
+        if not last:
+            offsets(0, B)
+            offsets(1, B)
+        else:
+            dma("A", ("yn", 0, L0), ("L", LP, LP + L0), "st2", 128 * L0 * 4)
+        LC = ("LC", 0, 128)
+        tt(LC, ("ind", Lw, MO), ("GG", 0, 128), Op.min)
+        if t:
+            cp(("ind", ("L", LP + L0, LP + LM), CO), LC)
+        else:
+            cp(("L", LP + L0, LP + L0 + CAP), LC)
+        if not last:
+            offsets(2, width(t + 1, 2))
+            w = width(t + 1, 2)
+            dma("S", (WN, G + L0, G + L0 + w), ("L", LP + L0, LP + L0 + w), "wt%d" % t, 128 * w * 4)
+        else:
+            dma("A", ("yn", L0, LM), ("L", LP + L0, LP + LM), "st3", 128 * (LM - L0) * 4)
+    return ops
+
+
+def schedule(ops, cfg=None):
+    cfg = cfg or CFG
+    n = len(ops)
+    succ = [[] for _ in range(n)]
+    for o in ops:
+        for d in o["deps"]:
+            succ[d].append(o["id"])
+
+    def span(o):
+        return o["cost"] + (o["lat"] + o["nbytes"] / cfg["bw"] if "nbytes" in o else 0.0)
+
+    prio = [0.0] * n
+    for o in reversed(ops):
+        prio[o["id"]] = span(o) + cfg["sem"] + max([prio[s] for s in succ[o["id"]]], default=0.0)
+    left = [len(o["deps"]) for o in ops]
+    ready_at = [0.0] * n
+    done = [0.0] * n
+    start = [0.0] * n
+    pool = {e: [] for e in "VAPGSX"}
+    free = {e: 0.0 for e in "VAPGS"}
+    state = {"dma": 0.0, "first": True}
+    order = {e: [] for e in "VAPGS"}
+    issued = set()
+
+    def release(i):
+        for s in succ[i]:
+            ready_at[s] = max(ready_at[s], done[i] + cfg["sem"])
+            left[s] -= 1
+            if left[s] == 0:
+                if ops[s]["eng"] == "X":
+                    start[s] = ready_at[s]
+                    done[s] = ready_at[s] + ops[s]["cost"]
+                    release(s)
+                else:
+                    pool[ops[s]["eng"]].append(s)
+
+    for o in ops:
+        if not o["deps"]:
+            pool[o["eng"]].append(o["id"])
+    while True:
+        best = None
+        for e in "VAPGS":
+            can = [i for i in pool[e] if all(j in issued for j in ops[i].get("soft", ()))]
+            if can:
+                tm = max(free[e], min(ready_at[i] for i in can))
+                if best is None or tm < best[0]:
+                    best = (tm, e, can)
+        if best is None:
+            break
+        tm, e, can = best
+        i = max((i for i in can if ready_at[i] <= tm + cfg["look"]), key=lambda j: (prio[j], -j))
+        tm = max(tm, ready_at[i])
+        pool[e].remove(i)
+        issued.add(i)
+        o = ops[i]
+        start[i] = tm
+        free[e] = tm + o["cost"]
+        if "nbytes" in o:
+            extra = 0.0
+            if e == "G" and state["first"]:
+                state["first"] = False
+                extra = cfg["first"]
+            s0 = max(free[e] + o["lat"] / 2 + extra, state["dma"])
+            state["dma"] = s0 + o["nbytes"] / cfg["bw"]
+            done[i] = state["dma"] + o["lat"] / 2
+        else:
+            done[i] = free[e]
+        order[e].append(i)
+        release(i)
+    return order, start, done
+
+
+PLAN = []
+
+
+def plan():
+    if not PLAN:
+        ops = build()
+        order, start, done = schedule(ops)
+        PLAN.append((ops, order, start, done))
+    return PLAN[0]
+
+
+def helper_program(g, core, owner, T, topo):
+    rid, pid, _ = topo.addr(owner)
+    m = topo.mask(core, owner)
+    sent = 0
+    for i, (t, c) in enumerate(INST):
+        if fold_units(t, c):
+            lo, hi = fold_cols(t, c)
+            g.wait_ge(T.sem["ha%d" % i], 16)
+            g.remote_dma(T.YZ[:, lo:hi], T.YZ[:, lo:hi], T.sem["ya%d" % i], T.sem.hback, pid, rid, m)
+            sent += len(topo.engines(core, owner))
+    g.wait_ge(T.sem.hback, sent)
+
+
+def rank_program(g, core, T, topo):
+    rank = T.rank_of(core)
+    if rank is None:
+        for c in T.cores:
+            if helper_of(c, T, topo) == core:
+                helper_program(g, core, c, T, topo)
+        return
+    ops, order, start, done = plan()
+    queue = {"V": g.vector, "A": g.scalar, "P": g.tensor, "G": g, "S": g.sync}
+    helper = helper_of(core, T, topo)
+
+    def ap(a):
+        if not isinstance(a, tuple):
+            return a
+        if a[0] == "ind":
+            return ap(a[1]).indirect(ap(a[2]))
+        if len(a) > 3:
+            return T[a[0]][:, a[1]:a[2]:a[3]]
+        return T[a[0]][:, a[1]:a[2]]
+
+    total = {}
+    for o in ops:
+        if "sem" in o:
+            total[o["sem"]] = total.get(o["sem"], 0) + o["inc"]
+    needed = set()
+    for o in ops:
+        needed |= o["deps"]
+    event = {}
+    for o in ops:
+        if "sem" in o:
+            event[o["id"]] = (o["sem"], total[o["sem"]])
+    for e in "VAPG":
+        k = 0
+        for i in order[e]:
+            if i not in event and i in needed:
+                k += 1
+                event[i] = (ESEM[e], k)
+        total[ESEM[e]] = k
+    first, lastin = {}, {}
+    for i in order["P"]:
+        gr = ops[i]["group"]
+        if gr is not None:
+            first.setdefault(gr, i)
+            lastin[gr] = i
+
+    def issue(q, o):
+        kind, a = o["kind"], o["args"]
+        if kind == "mm":
+            gr = o["group"]
+            return q.matmul(ap(a[0]), ap(a[1]), ap(a[2]), gr is None or first[gr] == o["id"], gr is None or lastin[gr] == o["id"])
+        if kind == "iota":
+            if SCRATCH[a[0][0]][2] == "int32":
+                return q.iota(ap(a[0]), a[1], a[2], a[3])
+            return q.iota(ap(a[0]), a[1], a[2], a[3], allow_small_or_imprecise_dtypes=True)
+        if kind == "dma":
+            if a[2] is None:
+                return q.dma_start(ap(a[0]), ap(a[1]))
+            return q.dma_start(T[a[0][0]][a[2]::16, a[0][1]:a[0][2]], T[a[1][0]][a[2]::16, a[1][1]:a[1][2]])
+        if kind == "send":
+            buf, t = a
+            trs = []
+            for d in range(2):
+                dst = T.cores[(rank - OFF[d]) % N]
+                rid, pid, _ = topo.addr(dst)
+                en = topo.engines(core, dst)
+                half = en[d * len(en) // 2:(d + 1) * len(en) // 2]
+                trs.append(RemoteDMATransfer(dst_ids=[DstId(rid=rid, pnc=pid)], dma_engine_mask=mask_of(half),
+                                             remote_sem=T.sem[("ga%d", "gb%d")[d] % t], src=T[buf][:, G:G + B], dst=T[buf][:, d * B:d * B + B]))
+            g.remote_dma_fused(trs, local_sem=T.sem[o["sem"]])
+            return None
+        if kind == "fold":
+            i, t, c = a
+            w = width(t, c)
+            us = fold_units(t, c)
+            rid, pid, _ = topo.addr(helper)
+            en = topo.engines(core, helper)
+            trs = []
+            for j, u in enumerate(us):
+                part = en[j * len(en) // len(us):(j + 1) * len(en) // len(us)]
+                lo = 2 * B * c + (0 if u == "y" else w)
+                trs.append(RemoteDMATransfer(dst_ids=[DstId(rid=rid, pnc=pid)], dma_engine_mask=mask_of(part), remote_sem=T.sem["ha%d" % i],
+                                             srcs=[T["P%d" % c][:, k * w:k * w + w] for k in range(16)], dsts=[T.YZ[:, lo:lo + w]],
+                                             alu_op=2 if u == "y" else 3))
+            g.remote_dma_fused(trs, local_sem=T.sem[o["sem"]])
+            return None
+        out, ins, x = a
+        if kind == "ts":
+            if x[1] is None:
+                return q.tensor_scalar(ap(out), ap(ins[0]), ap(ins[1]), None, x[0])
+            return q.tensor_scalar(ap(out), ap(ins[0]), ap(ins[1]), ap(ins[2]), x[0], x[1])
+        if kind == "tt":
+            return q.tensor_tensor(ap(out), ap(ins[0]), ap(ins[1]), x)
+        if kind == "cp":
+            return q.tensor_copy(ap(out), ap(ins[0]))
+        if kind == "tr":
+            return q.transpose(ap(out), ap(ins[0]))
+        if kind == "scan":
+            return q.tensor_tensor_scan(ap(out), ap(ins[0]), ap(ins[1]), 0.0, Op.mult, Op.add)
+        if x[1] is None:
+            return q.activation(ap(out), ap(ins[0]), x[0])
+        return q.activation(ap(out), ap(ins[0]), x[0], scale=x[1])
+
+    for e in "SAVPG":
+        q = queue[e]
+        known = {}
+        for i in order[e]:
+            o = ops[i]
+            want = {}
+            for d in o["deps"]:
+                s, v = event[d]
+                want[s] = max(want.get(s, 0), v)
+            for s, v in sorted(want.items()):
+                if known.get(s, 0) < v:
+                    q.wait_ge(T.sem[s], v)
+                    known[s] = v
+            ins = issue(q, o)
+            if ins is not None and i in event:
+                ins.then_inc(T.sem[event[i][0]], 16 if "sem" in o else 1)
+        if e == "G":
+            for s, v in sorted(total.items()):
+                if v and known.get(s, 0) < v:
+                    q.wait_ge(T.sem[s], v)

@@ -1,3 +1,4 @@
+import numpy as np
 from concourse.bass import DstId, RemoteDMATransfer
 from concourse.mybir import AluOpType, ActivationFunctionType
 
@@ -5,67 +6,83 @@ N = 4
 L0, CAP, RO, B, OFF, H = 768, 128, 4, 384, (3, 1), 72
 G = B * len(OFF)
 LM = L0 + RO * CAP
+LW = LM - CAP
 NP = G + LM
 VOID = NP - 1
-LP = 32
+NONE = LM + B
 BIG = 4096.0
+SHIFT = 1281.0
+WM = 512
+QS_N, QH_N = 11520, 3072
+CM = 64
 
 CFG = {
-    "KD": 10,
-    "KV": [[6, 0, 0], [3, 0, 0], [3, 0, 0], [3, 0, 0]],
-    "AS": "yz",
-    "look": 0.0,
-    "KC": 4,
-    "VU": {t: [(0, "z"), (1, "z"), (2, "z")] for t in range(4)},
-    "f": 1.2, "gath": 1.5, "scat": 3.8, "bw": 280.0, "fix": 40.0, "sem": 70.0, "rlat": 2200.0, "riss": 600.0,
-    "dlat": 1800.0, "diss": 120.0, "first": 2500.0,
+    "CH": [[(384, "f"), (384, "f")],
+           [(384, "f"), (384, "f"), (128, "f")],
+           [(384, "f"), (384, "f"), (256, "f")],
+           [(384, "f"), (384, "f"), (384, "f")]],
+    "KV": [[4, 0], [4, 0, 0], [4, 0, 0], [4, 0, 0]],
+    "QV": [[0, 0], [0, 0, 0], [0, 0, 0], [0, 0, 4]],
+    "QP": [[0, 0], [2, 0, 0], [0, 0, 0], [0, 0, 4]],
+    "TV": 2,
+    "KC": 4, "KQ": 3, "KW": 1,
+    "EG": True,
+    "ST": [768],
+    "dp0": 2000.0, "keep": False, "OV": [], "B3": {}, "NV": 128, "pad": [0.0, 0.0, 0.0, 0.0], "dpad": 0.0, "P75": True, "ZP": True, "NAT": True, "SA": "", "look": 0.0, "turns": 5,
+    "f": 1.15, "gath": 1.48, "scat": 3.2, "bw": 472.0, "row": 6.0, "fix": 15.0, "pfix": 30.0, "sem": 100.0, "rlat": 2600.0,
+    "riss": 600.0, "dlat": 1600.0, "diss": 120.0, "first": 2500.0, "gf": 1.08,
 }
 
-INST = [(t, c) for t in range(RO) for c in range(3) if (c < 2 or t > 0)]
+
+def chunks(t, cfg=CFG):
+    out, o0 = [], 0
+    for c, (w, how) in enumerate(cfg["CH"][t]):
+        out.append((c, o0, w, how))
+        o0 += w
+    return out
 
 
-def width(t, c):
-    return B if c < 2 else CAP * t
+def instances(cfg=CFG):
+    return [(t, c) for t in range(RO) for c in range(len(cfg["CH"][t]))]
 
 
+F32, BF, F16 = "float32", "bfloat16", "float16"
 SCRATCH = {
-    "X0": ("sbuf", [128, NP], "float32"), "X1": ("sbuf", [128, NP], "float32"),
-    "W0": ("sbuf", [128, NP], "float32"), "W1": ("sbuf", [128, NP], "float32"),
-    "L": ("sbuf", [128, LM + 2 * LP], "float32"),
+    "X0": ("sbuf", [128, G + NONE + 8], F32), "X1": ("sbuf", [128, G + NONE + 8], F32),
+    "FC": ("sbuf", [128, 8], F32), "DG": ("sbuf", [128, B], BF), "IDB": ("sbuf", [128, 128], BF),
+    "W0": ("sbuf", [128, NP], F32), "W1": ("sbuf", [128, NP], F32),
     "NB": ("sbuf", [128, L0], "int32"),
-    "P0": ("sbuf", [128, 16 * B], "float32"), "P1": ("sbuf", [128, 16 * B], "float32"), "P2": ("sbuf", [128, 16 * B], "float32"),
-    "Q0": ("sbuf", [128, 16 * B], "float32"), "Q1": ("sbuf", [128, 16 * B], "float32"),
-    "C0": ("sbuf", [128, 16 * B], "bfloat16"), "C1": ("sbuf", [128, 16 * B], "bfloat16"),
-    "QD": ("sbuf", [128, 3 * B], "float32"),
-    "YZ": ("sbuf", [128, 6 * B], "float32"),
-    "TR0": ("sbuf", [128, 2 * B + 32], "float32"), "TR1": ("sbuf", [128, 2 * B + 32], "float32"),
-    "OT": ("sbuf", [128, 3 * B], "uint16"),
-    "BV": ("sbuf", [128, 3 * B], "bfloat16"),
-    "T1": ("sbuf", [128, B], "float32"), "T3": ("sbuf", [128, 3 * B], "float32"), "T5": ("sbuf", [128, B], "float32"),
-    "PL": ("sbuf", [128, LM], "float32"),
-    "IM": ("sbuf", [128, 144], "float32"), "I2": ("sbuf", [128, 24], "float32"), "I16": ("sbuf", [128, 128], "float32"),
-    "PI": ("sbuf", [128, 8], "int32"), "CF": ("sbuf", [128, 16], "float32"), "NM": ("sbuf", [128, 16], "float32"),
-    "LS": ("sbuf", [128, 48], "uint16"),
-    "YB": ("sbuf", [128, 144], "bfloat16"), "ID": ("sbuf", [128, 128], "float32"), "NI": ("sbuf", [128, 128], "float32"),
-    "ND": ("sbuf", [128, 128 * max(1, 16 - CFG["KD"])], "float32"),
-    "TRI": ("sbuf", [128, 128], "bfloat16"), "ONE": ("sbuf", [128, 128], "bfloat16"), "E1": ("sbuf", [128, 128], "bfloat16"),
-    "BM": ("sbuf", [128, 128], "float32"), "MA": ("sbuf", [128, 8], "float32"), "WE": ("sbuf", [128, 8], "float32"),
-    "RR": ("sbuf", [128, 18], "bfloat16"),
-    "RB": ("sbuf", [128, 16], "bfloat16"), "RS": ("sbuf", [128, 16], "bfloat16"), "CR": ("sbuf", [128, 16], "float32"),
-    "HH": ("sbuf", [128, 9 * 128], "bfloat16"),
-    "ST": ("sbuf", [128, 32], "float32"), "RW": ("sbuf", [128, 8], "float32"),
-    "MO": ("sbuf", [128, 8], "uint16"), "CO": ("sbuf", [128, 8], "uint16"),
-    "KK": ("sbuf", [128, 128], "float32"), "CH": ("sbuf", [128, 128], "float32"), "FF": ("sbuf", [128, 128], "float32"),
-    "GG": ("sbuf", [128, 128], "float32"), "XM": ("sbuf", [128, 128], "float32"), "LA": ("sbuf", [128, 128], "float32"),
-    "LC": ("sbuf", [128, 128], "float32"),
-    "XP0": ("psum", [128, 512], "float32"), "XP1": ("psum", [128, 512], "float32"), "XP2": ("psum", [128, 512], "float32"),
-    "VL0": ("psum", [128, 512], "float32"), "VL1": ("psum", [128, 512], "float32"), "VL2": ("psum", [128, 512], "float32"),
-    "S0": ("psum", [128, 512], "float32"), "S1": ("psum", [128, 512], "float32"),
+    "OF": ("sbuf", [128, 48], F32), "OG": ("sbuf", [128, 48], F32), "BA": ("sbuf", [128, 8 * 128], F16),
+    "V1": ("sbuf", [128, 8], F32), "V2": ("sbuf", [128, 16], F16), "NR": ("sbuf", [128, 8], F32),
+    "P": ("sbuf", [128, 16 * LW], F32), "C": ("sbuf", [128, 24 * B], BF),
+    "QS": ("sbuf", [128, QS_N], F32), "QH": ("sbuf", [128, QH_N], F16), "QD": ("sbuf", [128, LW], F32),
+    "Y": ("sbuf", [128, LW], F32), "T3": ("sbuf", [128, LW], F32), "BV": ("sbuf", [128, LW], BF),
+    "T1": ("sbuf", [128, 2 * WM], F16),
+    "OT0": ("sbuf", [128, LW], "uint16"), "OT1": ("sbuf", [128, LW], "uint16"),
+    "PL": ("sbuf", [128, NONE + 8], F32),
+    "IM": ("sbuf", [128, 144], F32), "IB": ("sbuf", [128, 240], BF), "I16": ("sbuf", [128, 128], BF),
+    "PI": ("sbuf", [128, 8], "int32"), "CF": ("sbuf", [128, 16], F32), "NM": ("sbuf", [128, 16], F32),
+    "CG": ("sbuf", [128, 8], F32), "I2": ("sbuf", [128, 24], F32), "LS": ("sbuf", [128, 48], "uint16"),
+    "ZC": ("sbuf", [128, 8], F32), "ZZ": ("sbuf", [128, 9 * 128], F16), "R32": ("sbuf", [128, 24], F32),
+    "YB": ("sbuf", [128, 144], BF), "ID": ("sbuf", [128, 128], F32), "IQ": ("sbuf", [128, 128], F32), "IN": ("sbuf", [128, 128], F32),
+    "NI": ("sbuf", [128, 4 * 128], F32), "ND": ("sbuf", [128, 16 * 128], F32), "NH": ("sbuf", [128, 8 * 128], F16),
+    "TRI": ("sbuf", [128, 128], BF), "ONE": ("sbuf", [128, 128], BF), "HALF": ("sbuf", [128, 8], BF), "E1": ("sbuf", [128, 128], F16),
+    "BM": ("sbuf", [128, 128], F16), "MA": ("sbuf", [128, 8], F32), "WE": ("sbuf", [128, 8], F32),
+    "RR": ("sbuf", [128, 24], F16), "P2": ("sbuf", [128, 8], F32), "IV": ("sbuf", [128, 8], F16), "IDH": ("sbuf", [128, 128], F16),
+    "RB": ("sbuf", [128, 16], BF), "RS": ("sbuf", [128, 16], BF), "CR": ("sbuf", [128, 16], F32),
+    "HH": ("sbuf", [128, 9 * 128], F16),
+    "ST": ("sbuf", [128, 32], F32), "RW": ("sbuf", [128, 16], F16),
+    "MO": ("sbuf", [128, 16], "uint16"), "CO": ("sbuf", [128, 8], "uint16"),
+    "CH": ("sbuf", [128, 128], F32), "GG": ("sbuf", [128, 128], F32), "XM": ("sbuf", [128, 128], F32), "LA": ("sbuf", [128, 128], F32),
+    "XP0": ("psum", [128, 512], F32), "XP1": ("psum", [128, 512], F32), "XP2": ("psum", [128, 512], F32),
+    "VL0": ("psum", [128, 512], F32), "VL1": ("psum", [128, 512], F32),
+    "Z": ("psum", [128, 512], F32), "A": ("psum", [128, 512], F32), "S": ("psum", [128, 512], F32),
 }
 
-SEMAPHORES = (["eV", "eA", "eP", "eG", "hback"] + ["ld%d" % i for i in range(4)] + ["st%d" % i for i in range(4)] + ["wt%d" % i for i in range(RO - 1)]
+SEMAPHORES = (["eV", "eA", "eP", "eG", "hback"] + ["ld%d" % i for i in range(4)] + ["st%d" % i for i in range(8)]
+              + ["cp%d" % i for i in range(8)] + ["lc%d" % i for i in range(RO)]
               + ["gl%d" % i for i in range(RO)] + ["ga%d" % i for i in range(RO)] + ["gb%d" % i for i in range(RO)]
-              + ["%s%d" % (s, i) for s in ("fl", "ha", "ya", "dq") for i in range(len(INST))])
+              + ["%s%d" % (s, i) for s in ("fl", "ha", "ya", "dq") for i in range(len(instances()))])
 
 ESEM = {"V": "eV", "A": "eA", "P": "eP", "G": "eG"}
 Op = AluOpType
@@ -79,17 +96,6 @@ def helper_of(core, T, topo):
     return free[ranks.index(core) % len(free)]
 
 
-def fold_units(t, c):
-    return [u for u in ("y", "z") if (c, u) not in CFG["VU"].get(t, [])]
-
-
-def fold_cols(t, c):
-    w = width(t, c)
-    us = fold_units(t, c)
-    lo = 2 * B * c + (0 if "y" in us else w)
-    return lo, lo + w * len(us)
-
-
 def mask_of(engines):
     m = 0
     for e in engines:
@@ -97,13 +103,23 @@ def mask_of(engines):
     return m
 
 
-def build():
+def meet(r, s):
+    if r[1] >= s[2] or s[1] >= r[2]:
+        return False
+    if len(r) > 3 and len(s) > 3 and r[3] == s[3]:
+        return (r[1] - s[1]) % r[3] == 0
+    return True
+
+
+def build(cfg=CFG):
     ops = []
     hist = {}
     bysem = {}
+    inbank = {}
     late = []
-    cyc = 0.83 * CFG["f"]
-    KD, KC = CFG["KD"], CFG["KC"]
+    cyc = 0.83 * cfg["f"]
+    gcyc = 0.83 * cfg["gf"]
+    INST = instances(cfg)
 
     def psum(name):
         return name in SCRATCH and SCRATCH[name][0] == "psum"
@@ -117,12 +133,12 @@ def build():
         o = dict(id=len(ops), eng=eng, kind=kind, args=args, cost=cost, group=group, deps=set(after), **kw)
         acc = [(r, False) for r in reads] + [(r, True) for r in writes]
         for r, wr in acc:
-            for (lo, hi, oid, ow, oe, og) in hist.get(r[0], []):
+            for (s, oid, ow, oe, og) in hist.get(r[0], []):
                 if group is not None and og == group and wr and ow:
                     continue
                 if psum(r[0]) and oe != eng:
                     o["deps"].add(oid)
-                elif (wr or ow) and lo < r[2] and r[1] < hi:
+                elif (wr or ow) and meet(r, s):
                     o["deps"].add(oid)
         for d in list(o["deps"]):
             if "sem" in ops[d]:
@@ -132,8 +148,13 @@ def build():
         for r, wr in acc:
             h = hist.setdefault(r[0], [])
             if wr and group is None and len(r) == 3 and not psum(r[0]) and not kw.get("part"):
-                h[:] = [x for x in h if not (r[1] <= x[0] and x[1] <= r[2])]
-            h.append((r[1], r[2], o["id"], wr, eng, group))
+                h[:] = [x for x in h if not (r[1] <= x[0][1] and x[0][2] <= r[2])]
+            if psum(r[0]) and h and h[-1][3] != eng:
+                j = len(h)
+                while j and h[j - 1][3] != eng:
+                    j -= 1
+                del h[:j]
+            h.append((r, o["id"], wr, eng, group))
         ops.append(o)
         return o["id"]
 
@@ -143,7 +164,7 @@ def build():
         return len(range(a[1], a[2], a[3] if len(a) > 3 else 1))
 
     def two(a):
-        return SCRATCH[a[0]][2] in ("bfloat16", "uint16")
+        return SCRATCH[a[0]][2] in (BF, F16, "uint16")
 
     def comp(eng, kind, out, ins, args, mult=1.0):
         reads, writes = [], []
@@ -153,13 +174,13 @@ def build():
         part = False
         if out[0] == "ind":
             writes.append(out[1]); reads.append(out[2]); part = True
-            cost = 50 + nel(out) * CFG["scat"] * cyc
+            cost = 50 + nel(out) * cfg["scat"] * gcyc
         else:
             writes.append(out)
             if isinstance(ins[0], tuple) and ins[0][0] == "ind":
-                cost = (50 if eng == "V" else 65) + nel(out) * CFG["gath"] * cyc
+                cost = (50 if eng == "V" else 65) + nel(out) * cfg["gath"] * gcyc
             else:
-                cost = CFG["fix"] + max(64, nel(out) * mult) * cyc
+                cost = cfg["fix"] + max(64, nel(out) * mult) * cyc
         return add(eng, kind, (out, ins, args), reads, writes, cost, part=part)
 
     def ts(out, a, s1, op0, s2=None, op1=None):
@@ -173,279 +194,431 @@ def build():
     def cp(out, a):
         return comp("V", "cp", out, [a], None)
 
-    def act(out, a, fn, scale=None):
-        return comp("A", "act", out, [a], (fn, scale))
+    def act(out, a, fn, scale=None, bias=None):
+        return comp("A", "act", out, [a, bias, scale], fn)
 
-    def mm(out, lhs, rhs, group=None):
-        k = 4 if SCRATCH[rhs[0]][2] == "float32" else 1
-        return add("P", "mm", (out, lhs, rhs), [lhs, rhs], [out], 15 + max(64, nel(rhs)) * k * cyc / 2, group=group)
+    def scale(tag, out, a, s):
+        return act(out, a, Fn.Copy, s) if tag in cfg["SA"] else ts(out, a, s, Op.mult)
+
+    def mm(out, lhs, rhs, group=None, behind=()):
+        k = 4 if SCRATCH[rhs[0]][2] == F32 else 1
+        prev = inbank.setdefault(out[0], [])
+        soft = [j for j in prev if group is None or ops[j]["group"] != group] + list(behind)
+        j = add("P", "mm", (out, lhs, rhs), [lhs, rhs], [out], cfg["pfix"] + max(64, nel(rhs)) * k * cyc / 2, group=group, soft=soft)
+        prev[:] = prev[-40:] + [j]
+        return j
 
     def iota(out, pattern, base, cm=0):
         return add("G", "iota", (out, pattern, base, cm), [], [out], 130 + 2 * nel(out) * cyc, soft=list(late))
 
+    def select(out, a, pattern, op, val, base, cm):
+        return add("G", "select", (out, a, pattern, op, val, base, cm), [a], [out], 170 + 2 * nel(out) * cyc, soft=list(late))
+
     def fill(out, val):
         return iota(out, [[0, nel(out)]], val)
 
-    def dma(eng, out, a, sem, nbytes, group=None, rows=None):
-        return add(eng, "dma", (out, a, rows), [a], [out], CFG["diss"], group=group, sem=sem, inc=16, nbytes=nbytes, lat=CFG["dlat"],
-                   part=rows is not None)
+    def dma(eng, out, a, sem, group=None, rows=None):
+        n = 128 if rows is None else 8
+        return add(eng, "dma", (out, a, rows), [a], [out], cfg["diss"], group=group, sem=sem, inc=16, lat=cfg["dlat"] + (cfg["dpad"] if rows is not None else 0.0),
+                   busy=n * nel(a) * 4 / cfg["bw"] + max(n, 16) * cfg["row"] / 16, part=rows is not None)
 
     def send(t, buf):
-        s = add("G", "send", (buf, t), [(buf, G, G + B)], [], CFG["riss"], sem="gl%d" % t, inc=16, nbytes=2 * 128 * B * 4, lat=CFG["rlat"])
+        s = add("G", "send", (buf, t), [(buf, G, G + B)], [], cfg["riss"], sem="gl%d" % t, inc=16, lat=cfg["rlat"],
+                busy=2 * 128 * B * 4 / cfg["bw"] + 16 * cfg["row"])
         if t == 0:
             late.append(s)
         for d in range(2):
             add("X", "arrive", None, [], [(buf, d * B, d * B + B)], 300.0, after=[s], sem=("ga%d", "gb%d")[d] % t, inc=8)
+        return s
 
     def col(name, j):
         return (name, j, j + 1)
 
+    def blk(name, j):
+        return (name, 128 * j, 128 * j + 128)
+
     E = ("IM", 15, 143)
+    ID, IQ, IN = blk("ID", 0), blk("IQ", 0), blk("IN", 0)
 
     def esl(n):
         return ("IM", 15, 15 + n)
 
-    cP, cB, cG, cPB, cE, cHB, cDF, cC1, cD8, cD24, cND = [col("CF", j) for j in range(11)]
+    cP, cB, cG, cND, cB113 = [col("CF", j) for j in range(5)]
+    cVB = col("P2", 4)
 
-    dma("S", ("X0", G, G + B), ("x0", 0, B), "ld0", 128 * B * 4)
-    dma("A", ("NB", 0, B), ("nb", 0, B), "ld1", 128 * B * 4)
-    dma("A", ("NB", B, L0), ("nb", B, L0), "ld2", 128 * B * 4)
-    dma("S", ("X0", G + B, G + L0), ("x0", B, L0), "ld3", 128 * B * 4)
+    def split(t, c):
+        ks = 16 - cfg["QV"][t][c]
+        return ks - cfg["QP"][t][c], ks
+
+    def natural(t, c):
+        return cfg["NAT"] and t == 0 and c == 0
+
+    rest = [(t, c) for t, c in INST if not natural(t, c)]
+    kds = sorted(set(split(t, c)[0] for t, c in rest) - {0})
+    nds = list(range(16)) if cfg["NAT"] else sorted(set(k for t, c in rest for k in range(*split(t, c))))
+    nhs = sorted(set(k for t, c in rest for k in range(split(t, c)[1], 16)))
+
+    dma("A", ("NB", 0, B), ("nb", 0, B), "ld1")
+    dma("S", ("X0", G, G + B), ("x0", 0, B), "ld0")
+    dma("A", ("NB", B, L0), ("nb", B, L0), "ld2")
+    dma("S", ("X0", G + B, G + L0), ("x0", B, L0), "ld3")
     iota(("PI", 0, 1), [[0, 1]], 0, 1)
     iota(("IM", 0, 144), [[1, 144]], -15)
-    iota(("I2", 0, 24), [[256, 3], [2, 8]], 0)
-    fill(("L", 0, LP), 0)
-    fill(("L", LP + L0, LP + L0 + LP), VOID)
+    if cfg["OV"]:
+        iota(("I2", 0, 24), [[256, 3], [2, 8]], 0)
+    iota(("IB", 0, 128), [[1, 128]], 0)
+    for j in range(2):
+        iota(("W0", B * j, B * j + B), [[1, B]], B * j)
     send(0, "X0")
-    late.append(iota(("W0", 0, G), [[1, G]], 0))
-    fill(("L", LP + L0 + LP, LP + LM - CAP), VOID)
-    fill(("L", LP + LM - CAP, LM + 2 * LP), 0)
     fill(("W0", G + L0, NP), VOID)
-    fill(("X0", G + L0, NP), 0)
-    fill(("QD", 0, 3 * B), 0)
     fill(("X1", G + L0, NP), 0)
+    dma("S", ("X0", G + L0, NP), ("X1", G + L0, NP), "cp0")
+    for j in range(3):
+        dma("S", ("QD", B * j, B * j + B), ("X1", G + L0, G + L0 + B), "cp1", group="qd")
+    dma("S", ("W1", 0, G), ("W0", 0, G), "cp2")
+    dma("S", ("W1", G + L0, NP), ("W0", G + L0, NP), "cp3")
     iota(("I16", 0, 128), [[0, 8], [1, 16]], 0)
     fill(("ONE", 0, 128), 1)
     fill(("RB", 0, 16), 0)
     fill(("RS", 0, 16), 0)
     fill(("ST", 0, 1), L0)
-    iota(("PL", 0, LM), [[1, LM]], G)
-    iota(("W1", 0, G), [[1, G]], 0)
-    fill(("W1", G + L0, NP), VOID)
+    for j in range(0, LM, 320):
+        iota(("PL", j, j + 320), [[1, 320]], G + j)
+    iota(("PL", LM, NONE), [[1, B]], G)
+    fill(("PL", NONE, NONE + 8), VOID)
+    for buf in ("X0", "X1"):
+        fill((buf, G + NONE, G + NONE + 8), 0)
     p0 = col("PI", 0)
     ts(col("PI", 1), p0, 15, Op.bitwise_and)
     ts(col("PI", 2), p0, 112, Op.bitwise_and)
-    ts(col("PI", 3), p0, 1, Op.bitwise_and)
-    ts(col("PI", 4), p0, 4, Op.logical_shift_right, 1, Op.bitwise_and)
-    ts(col("PI", 5), p0, 3, Op.logical_shift_right, 1, Op.bitwise_and)
-    cp(("CF", 0, 6), ("PI", 0, 6))
-    ts(cDF, cPB, cE, Op.not_equal, float(B + 16), Op.mult)
-    ts(cC1, cB, 16.0, Op.mult, cDF, Op.add)
-    ts(cD24, cHB, float(1 - B), Op.mult, cC1, Op.add)
-    ts(("LS", 0, 24, 3), ("I2", 0, 8), cC1, Op.add)
-    ts(("LS", 1, 24, 3), ("I2", 8, 16), cD24, Op.add)
-    ts(("LS", 2, 24, 3), ("I2", 16, 24), cC1, Op.add, float(1 - B), Op.add)
-    ts(cD8, cHB, -127.0, Op.mult, cC1, Op.add)
-    ts(("LS", 24, 32), ("I2", 0, 8), cD8, Op.add)
-    ts(("LS", 32, 48), esl(16), cC1, Op.add)
-    lists = {B: ("LS", 0, 24), 128: ("LS", 24, 32), 256: ("LS", 32, 48)}
-    ts(("ID", 0, 128), E, cP, Op.is_equal)
+    cp(("CF", 0, 3), ("PI", 0, 3))
+    ts(ID, E, cP, Op.is_equal)
+    ts(("MA", 0, 8), esl(8), 16.0, Op.mult, cG, Op.is_equal)
+    ts(cB113, cB, 113.0, Op.add)
+    ts(("ZC", 0, 8), ("MA", 0, 8), cB113, Op.mult, -1.0, Op.add)
+    for a in range(9):
+        ts(blk("ZZ", a), ("IB", 0, 128), col("ZC", a) if a < 8 else -1.0, Op.is_equal)
     ts(("YB", 0, 144), ("IM", 0, 144), cG, Op.is_equal, BIG, Op.mult)
     ts(("NM", 0, 16), esl(16), cB, Op.is_equal, -1.0, Op.mult)
-    for k in range(KD, 16):
-        ts(("ND", 128 * (k - KD), 128 * (k - KD + 1)), E, cP, Op.is_equal, col("NM", k), Op.mult)
-    if KD:
-        ts(cND, cB, float(KD), Op.is_lt, -1.0, Op.mult)
-        ts(("NI", 0, 128), E, cP, Op.is_equal, cND, Op.mult)
-    ts(("TRI", 0, 128), E, cP, Op.is_ge)
-    ts(("E1", 0, 128), E, 1.0, Op.add)
+    act(IQ, ID, Fn.Copy, 0.25)
+    act(IN, ID, Fn.Copy, -0.75 if cfg["P75"] else -1.0)
+    for k in nds:
+        act(blk("ND", k), ID, Fn.Copy, col("NM", k))
+    for k in nhs:
+        ts(blk("NH", k - 8), E, cP, Op.is_equal, col("NM", k), Op.mult)
+    for j, kd in enumerate(kds):
+        ts(col("CF", 9 + j), cB, float(kd), Op.is_lt, -1.0, Op.mult)
+        scale("n", blk("NI", j), ID, col("CF", 9 + j))
+    select(blk("TRI", 0), blk("ONE", 0), [[1, 128]], Op.is_ge, 0.0, 0, -1)
+    select(blk("TRI", 0), blk("TRI", 0), [[1, 128]], Op.not_equal, 1.0 - SHIFT, 0, -1)
+    ts(("E1", 0, 128), E, 1.0 - SHIFT, Op.add)
     ts(("BM", 0, 128), ("I16", 0, 128), cB, Op.is_equal)
-    ts(("MA", 0, 8), esl(8), 16.0, Op.mult, cG, Op.is_equal)
+    for a in range(8):
+        ts(blk("BA", a), ("I16", 0, 128), cB, Op.is_equal, col("MA", a), Op.mult)
+    ts(("NR", 0, RO), esl(RO), cB, Op.is_equal)
+    ts(("NR", RO, 2 * RO), esl(RO), cB, Op.not_equal)
     ts(("WE", 0, 8), esl(8), 16.0, Op.mult, cB, Op.add)
-    ts(("RR", 0, 18, 2), esl(9), 0.0, Op.mult, cP, Op.add)
-    ts(("RR", 1, 18, 2), esl(9), 128.0, Op.mult)
-    for c in range(2):
-        cp(("L", LP + B * c, LP + B * c + B), ("NB", B * c, B * c + B))
-        act(("W0", G + B * c, G + B * c + B), ("L", LP + B * c, LP + B * c + B), Fn.Copy)
+    iota(("R32", 0, 6), [[128, 3], [LM, 2]], 0, 1)
+    iota(("R32", 6, 18), [[128, 6], [0, 2]], B, 1)
+    cp(("RR", 0, 18), ("R32", 0, 18))
+    iota(col("P2", 0), [[0, 1]], 0, 1)
+    fill(col("P2", 1), int(G - 1 + SHIFT - NP))
+    cp(blk("IDH", 0), ID)
+    if cfg["EG"]:
+        act(blk("IDB", 0), ID, Fn.Copy)
+    select(col("HALF", 0), col("ONE", 0), [[0, 1]], Op.is_equal, 0.5, 1, 0)
+    select(cVB, col("P2", 0), [[0, 1]], Op.is_equal, -(1.5 + 2.0 ** -23), 1, 0)
 
-    ntr = [0]
-    prevq = []
+    lists = {B: ("LS", 0, 24), 128: ("LS", 24, 32), 256: ("LS", 32, 48)}
+    widths = set(w for t in range(RO) for c, o0, w, how in chunks(t, cfg) if (t, o0) in cfg["OV"])
+    if widths:
+        cPB, cE, cHB, cDF, cC1, cD8, cD24 = [col("CG", j) for j in range(7)]
+        ts(col("PI", 3), p0, 1, Op.bitwise_and)
+        ts(col("PI", 4), p0, 4, Op.logical_shift_right, 1, Op.bitwise_and)
+        ts(col("PI", 5), p0, 3, Op.logical_shift_right, 1, Op.bitwise_and)
+        cp(("CG", 0, 3), ("PI", 3, 6))
+        ts(cDF, cPB, cE, Op.not_equal, float(B + 16), Op.mult)
+        ts(cC1, cB, 16.0, Op.mult, cDF, Op.add)
+        if B in widths:
+            ts(cD24, cHB, float(1 - B), Op.mult, cC1, Op.add)
+            ts(("LS", 0, 24, 3), ("I2", 0, 8), cC1, Op.add)
+            ts(("LS", 1, 24, 3), ("I2", 8, 16), cD24, Op.add)
+            ts(("LS", 2, 24, 3), ("I2", 16, 24), cC1, Op.add, float(1 - B), Op.add)
+        if 128 in widths:
+            ts(cD8, cHB, -127.0, Op.mult, cC1, Op.add)
+            ts(("LS", 24, 32), ("I2", 0, 8), cD8, Op.add)
+        if 256 in widths:
+            ts(("LS", 32, 48), esl(16), cC1, Op.add)
 
-    def offsets(c, w):
-        tr = "TR%d" % (ntr[0] % 2)
-        ntr[0] += 1
-        c0 = LP + B * c
-        comp("V", "tr", (tr, 0, w), [("L", c0, c0 + w)], None)
-        comp("V", "tr", (tr, B, B + w + 32), [("L", c0 - 16, c0 + w + 16)], None)
-        cp(("OT", B * c, B * c + w), ("ind", (tr, 0, B + w + 32), lists[w]))
+    nof = [0]
 
-    def xcopy(buf, c, w):
-        mm(("XP%d" % c, 0, w), ("ID", 0, 128), (buf, G + B * c, G + B * c + w))
+    def offsets(t, W, o0, w, bank, mend=False):
+        nb, A = w // 128, w // 16
+        q = WM * (nof[0] % 2)
+        nof[0] += 1
+        OT = "OT%d" % (t % 2)
+        if (t, o0) in cfg["OV"]:
+            q = take("QS", B + WM)
+            comp("V", "tr", ("QS", q, q + w), [(W, G + o0, G + o0 + w)], None)
+            comp("V", "tr", ("QS", q + B, q + B + w + 32), [(W, G + o0 - 16, G + o0 + w + 16)], None)
+            cp((OT, o0, o0 + w), ("ind", ("QS", q, q + B + w + 32), lists[w]))
+        else:
+            for b in range(nb):
+                mm((bank, b, w, nb), (W, G + o0 + 128 * b, G + o0 + 128 * b + 128), ID)
+            cp(("T1", q, q + w), (bank, 0, w))
+            for a in range(8):
+                for g in range(8):
+                    s = 128 * a + 112 - 16 * g
+                    mm((bank, a, w, 8), ("ZZ", s, s + 128), ("T1", q + 16 * nb * g, q + 16 * nb * (g + 1)), group=("ot", t, o0, a))
+            cp((OT, o0, o0 + w), (bank, 0, w))
+        if mend:
+            k, f = t - 1, o0 // 16
+            cp(("OF", f, f + A), (OT, o0 + k * A, o0 + k * A + A))
+            tt(("OG", f, f + A), ("OF", f, f + A), ("S", CM + f, CM + f + A), Op.max)
+            cp((OT, o0 + k * A, o0 + k * A + A), ("OG", f, f + A))
 
-    def kcalls(lo, hi):
+    def xp(t, c):
+        bank, at = 0, 0
+        for j, o0, w, how in chunks(t, cfg):
+            if at + w > WM:
+                bank, at = bank + 1, 0
+            if j == c:
+                return ("XP%d" % bank, at, at + w)
+            at += w
+
+    def vl(t, c):
+        if c == 2 and t in cfg["B3"]:
+            return cfg["B3"][t]
+        return "XP0" if t == RO - 1 and c == 2 and xp(t, 1)[0] != "XP0" else "VL%d" % (INST.index((t, c)) % 2)
+
+    def xcopy(t, buf, c, o0, w):
+        mm(xp(t, c), ID, (buf, G + o0, G + o0 + w))
+
+    def kcalls(lo, hi, most):
         n = hi - lo
         if n <= 0:
             return []
-        m = (n + KC - 1) // KC
+        m = (n + most - 1) // most
         cuts = [lo + (n * i) // m for i in range(m + 1)]
         return list(zip(cuts[:-1], cuts[1:]))
 
-    for c in range(2):
-        offsets(c, B)
-        xcopy("X0", c, B)
+    ring = {"QS": 0, "QH": 0, "C": 0}
 
+    def take(name, n):
+        if ring[name] + n > SCRATCH[name][1][1]:
+            ring[name] = 0
+        ring[name] += n
+        return ring[name] - n
+
+    for c, o0, w, how in chunks(0, cfg):
+        cp(("W0", G + o0, G + o0 + w), ("NB", o0, o0 + w))
+        if natural(0, c):
+            cp(("OT1", 0, w), ("NB", 0, w))
+    for c, o0, w, how in chunks(0, cfg):
+        offsets(0, "W0", o0, w, "VL%d" % (c % 2))
+        xcopy(0, "X0", c, o0, w)
+
+    prevq, folds = [], []
     for t in range(RO):
         X, XN, W, WN = "X%d" % (t % 2), "X%d" % (1 - t % 2), "W%d" % (t % 2), "W%d" % (1 - t % 2)
-        chunks = [c for c in range(3) if width(t, c)]
+        OT = "OT%d" % (t % 2)
+        chs = chunks(t, cfg)
         nb = (L0 + CAP * t) // 128
         cN, cNN = col("ST", t), col("ST", t + 1)
-        cNPE, cTR, cINV, cMM = [col("ST", 8 + j) for j in range(4)]
+        cNPE, cNH = col("ST", 8), col("ST", 9)
         last = t == RO - 1
         top = NP if t else G + L0
         if last:
             fill((W, VOID, NP), 0)
-        ts(cNPE, cN, cP, Op.add)
+            fill((WN, G + LW, NP), 0)
+            fill(("PL", NONE, NONE + 8), 0)
+        ts(("ST", 8, 10), ("P2", 0, 2), cN, Op.add)
         if t:
             ts(("CO", 0, 8), ("WE", 0, 8), cN, Op.add, float(-L0), Op.add)
-        ts(("CH", 0, 128), E, cN, Op.add, float(G), Op.add)
-        for c in chunks:
-            i = INST.index((t, c))
-            w = width(t, c)
+        ts(("CH", 0, 128), ("PL", 0, 128), cN, Op.add, col("NR", t), Op.mult)
+        early = cfg["EG"] and not last
+        c1, c2, c3 = 16, 32, 48
+        jb, ne = 0, L0 // 128
+        cat, reads_x = {}, []
+        for c, o0, w, how in chs:
             A = w // 16
-            Pb, Cb, XP = "P%d" % c, "C%d" % (i % 2), ("XP%d" % c, 0, w)
-            o0 = B * c
+            XP = xp(t, c)
+            tail = c >= len(chs) - cfg["TV"]
 
             def sl(buf, k0, k1=None):
-                return (buf, k0 * w, (k0 + 1 if k1 is None else k1) * w)
+                return (buf, 16 * o0 + k0 * w, 16 * o0 + (k0 + 1 if k1 is None else k1) * w)
 
-            KV = CFG["KV"][t][c]
-            for k0, k1 in kcalls(0, KV):
-                cp(sl(Pb, k0, k1), ("ind", (X, 0, top), ("OT", o0 + k0 * A, o0 + k1 * A)))
-            for k0, k1 in kcalls(KV, 16):
-                act(sl(Pb, k0, k1), ("ind", (X, 0, top), ("OT", o0 + k0 * A, o0 + k1 * A)), Fn.Copy)
-            us = fold_units(t, c)
-            if us:
-                lo, hi = fold_cols(t, c)
-                f = add("G", "fold", (i, t, c), [(Pb, 0, 16 * w)], [("YZ", lo, hi)], CFG["riss"], sem="fl%d" % i, inc=16,
-                        nbytes=len(us) * 16 * 128 * w * 4, lat=CFG["rlat"])
-                add("X", "arrive", None, [], [("YZ", lo, hi)], CFG["riss"] + CFG["rlat"] + 128 * (hi - lo) * 4 / CFG["bw"] + 300, after=[f],
+            KV = cfg["KV"][t][c]
+            for k0, k1 in kcalls(16 - KV, 16, cfg["KW"])[::-1]:
+                reads_x.append(cp(sl("P", k0, k1), ("ind", (X, 0, top), (OT, o0 + k0 * A, o0 + k1 * A))))
+            for k0, k1 in kcalls(0, 16 - KV, cfg["KC"])[::-1]:
+                reads_x.append(act(sl("P", k0, k1), ("ind", (X, 0, top), (OT, o0 + k0 * A, o0 + k1 * A)), Fn.Copy))
+            Y, T3, Z, Z2, AC = ("Y", o0, o0 + w), ("T3", o0, o0 + w), ("Z", 0, w), ("Z", 256, 256 + w), ("A", 0, w)
+            if how == "f":
+                i = INST.index((t, c))
+                f = add("G", "fold", (i, o0, w), [sl("P", 0, 16)], [Y], cfg["riss"], sem="fl%d" % i, inc=16, lat=cfg["rlat"],
+                        busy=16 * 128 * w * 4 / cfg["bw"] + 128 * cfg["row"], soft=folds[-1:])
+                folds.append(f)
+                add("X", "arrive", None, [], [Y], cfg["riss"] + cfg["rlat"] + 128 * w * 4 / cfg["bw"] + 8 * cfg["row"] + 300 + cfg["pad"][len(chs) - 1 - c], after=[f],
                     sem="ya%d" % i, inc=16)
-            for k in range(16):
-                tt(sl(Cb, k), sl(Pb, k), XP, Op.is_gt)
-                mm(("VL%d" % c, 0, w), ("YB", 15 - k, 143 - k), sl(Cb, k), group=("vl", i))
-            T3 = T4 = ("T3", o0, o0 + w)
-            T1, T2, T5, S0 = ("T1", 0, w), ("S1", 0, w), ("T5", 0, w), ("S0", 0, w)
-            for u in ("z", "y"):
-                if u in us:
-                    src = ("YZ", 2 * o0, 2 * o0 + w) if u == "y" else ("YZ", 2 * o0 + w, 2 * o0 + 2 * w)
-                else:
-                    op = Op.max if u == "y" else Op.min
-                    tt(S0, sl(Pb, 0), sl(Pb, 1), op)
-                    for k in range(2, 16):
-                        tt(S0, sl(Pb, k), S0, op)
-                    src = S0
-                if u == "z":
-                    tt(T3, src, XP if u in us else (X, G + o0, G + o0 + w), Op.mult)
-                    if "z" in CFG["AS"] and c != chunks[-1]:
-                        act(T4, T3, Fn.Copy, 0.75)
-                    else:
-                        ts(T4, T3, 0.75, Op.mult)
-                elif "y" in CFG["AS"] and u in us and c != chunks[-1]:
-                    act(T1, src, Fn.Copy, 0.25)
-                else:
-                    ts(T1, src, 0.25, Op.mult)
-            tt(T2, T1, XP, Op.add)
-            tt(T5, T2, T4, Op.subtract)
-            ts(("BV", o0, o0 + w), T5, 1.0, Op.is_gt)
-            ts((XN, G + o0, G + o0 + w), T5, 0.0, Op.max, 2.0, Op.min)
-            for j in range(o0 // 128, (o0 + w) // 128):
-                mm(col("S1", B + j), ("BV", 128 * j, 128 * j + 128), ("ONE", 0, 1))
-        for c in chunks:
-            i = INST.index((t, c))
-            w = width(t, c)
-            A = w // 16
-            Qb = "Q%d" % (i % 2)
-            o0 = B * c
-            for k0, k1 in kcalls(KD, 16) + kcalls(0, KD):
-                j = act((Qb, k0 * w, k1 * w), ("ind", (W, 0, top), ("OT", o0 + k0 * A, o0 + k1 * A)), Fn.Abs)
-                ops[j]["soft"] = prevq[-1:]
-                prevq.append(j)
-            for k in range(KD):
-                dma("S", ("QD", o0, o0 + w), (Qb, k * w, k * w + w), "dq%d" % i, 8 * w * 4, group=("dq", i), rows=k)
-            for k in range(KD, 16):
-                mm(("VL%d" % c, 0, w), ("ND", 128 * (k - KD), 128 * (k - KD + 1)), (Qb, k * w, k * w + w), group=("vl", i))
-            if KD:
-                mm(("VL%d" % c, 0, w), ("NI", 0, 128), ("QD", o0, o0 + w), group=("vl", i))
-        c0, c1, c2, c3 = B, B + 16, B + 32, B + 48
-        ts(("RB", 0, nb), ("S1", c0, c0 + nb), float(H), Op.is_ge)
-        comp("V", "scan", ("RS", 1, nb + 1), [("ONE", 0, nb), ("RB", 0, nb)], None)
-        mm(("S1", c1, c1 + nb + 1), ("TRI", 0, 128), ("RB", 0, nb + 1), group=("c", t))
-        mm(("S1", c1, c1 + nb + 1), ("ONE", 0, 128), ("RS", 0, nb + 1), group=("c", t))
-        tot = col("S1", c1 + nb)
-        tt(("CR", 0, nb), ("S1", c1, c1 + nb), ("RB", 0, nb), Op.mult)
-        ts(cINV, cP, tot, Op.is_ge, cNPE, Op.mult)
-        ts(cTR, tot, col("NM", t), Op.mult, -1.0, Op.mult)
+            if cfg["ZP"]:
+                mm(Z, ID, sl("P", 15))
+            if how == "v":
+                mm(Z2, ID, sl("P", 15))
+            for k in range(14, -1, -1):
+                tt(Z, sl("P", k), Z if cfg["ZP"] or k < 14 else sl("P", 15), Op.min)
+                if how == "v":
+                    tt(Z2 if k else Y, sl("P", k), Z2, Op.max)
+            for k in range(15, -1, -1):
+                cat[c, k] = take("C", w)
+                tt(("C", cat[c, k], cat[c, k] + w), sl("P", k), XP, Op.is_gt)
+                if c < 2 or vl(t, c) not in ("VL0", "VL1"):
+                    mm((vl(t, c), 0, w), ("YB", 15 - k, 143 - k), ("C", cat[c, k], cat[c, k] + w), group=("vl", INST.index((t, c))))
+            tt(T3, (X, G + o0, G + o0 + w), Z, Op.mult)
+            if cfg["P75"]:
+                pass
+            elif tail:
+                ts(T3, T3, 0.75, Op.mult)
+            else:
+                act(T3, T3, Fn.Copy, 0.75)
+            gr = ("x", t, c)
+            j0 = mm(AC, ID, (X, G + o0, G + o0 + w), group=gr)
+            j1 = mm(AC, IQ, Y, group=gr, behind=[j0])
+            mm(AC, IN, T3, group=gr, behind=[j1])
+            if tail:
+                ts(("BV", o0, o0 + w), AC, 1.0, Op.is_gt, -0.5, Op.add)
+            mid = min(max(B, o0), o0 + w) if early else o0
+            for at, lo, hi in ((NP, o0, mid), (G, mid, o0 + w)):
+                if lo < hi:
+                    ts((XN, at + lo, at + hi), ("A", lo - o0, hi - o0), 0.0, Op.max, 2.0, Op.min)
+                    if not tail:
+                        act(("BV", lo, hi), (XN, at + lo, at + hi), Fn.Sign, 1.5, cVB)
+            j1 = (o0 + w) // 128
+            for j in range(o0 // 128, j1):
+                mm(col("S", j), blk("BV", j), col("ONE" if tail else "HALF", 0))
+            ghosts = early and o0 < B <= o0 + w
+            if j1 < nb and not (o0 + w in cfg["ST"] or ghosts):
+                continue
+            je = j1 + (j1 == nb)
+            ts(("RB", jb, j1), ("S", jb, j1), float(H - 64), Op.is_ge)
+            comp("V", "scan", ("RS", jb + 1, j1 + 1), [("ONE", jb, j1), ("RB", jb, j1), col("RS", jb) if jb else 0.0], None)
+            mm(("S", c1 + jb, c1 + je), ("TRI", 0, 128), ("RB", jb, je), group=("c", t, c))
+            mm(("S", c1 + jb, c1 + je), ("ONE", 0, 128), ("RS", jb, je), group=("c", t, c))
+            jv = min(j1, ne)
+            if not last and jb < jv:
+                ts(("V2", jb, jv), ("S", c1 + jb, c1 + jv), CAP + 0.5 - SHIFT, Op.is_lt, float(NP), Op.mult)
+            if ghosts:
+                ts(("FC", 0, B // 128), ("V2", 0, B // 128), -0.5 / NP, Op.mult, 1.0, Op.add)
+                for j in range(B // 128):
+                    scale("d", blk("DG", j), blk("IDB", 0), col("FC", j))
+                    mm(blk("A", j), blk("ONE", 0), blk("DG", j))
+                tt((XN, G, G + B), (XN, NP, NP + B), ("A", 0, B), Op.mult)
+                sent = send(t + 1, XN)
+            for j in range(jb, j1):
+                ts(blk("HH", j), ("E1", 0, 128), col("S", c1 + j), Op.is_equal)
+            jb = j1
+        if early:
+            ops[sent]["deps"].update(reads_x)
+        tot = col("S", c1 + nb)
+        ts(col("IV", 0), cP, tot, Op.is_ge, cNPE, Op.mult)
+        ts(col("IV", 1), cP, tot, Op.is_ge, float(NONE), Op.mult)
         if not last:
             ts(cNN, tot, float(CAP), Op.min, cN, Op.add)
         for j in range(nb):
-            ts(("HH", 128 * j, 128 * j + 128), ("E1", 0, 128), col("CR", j), Op.is_equal)
-        for j in range(nb):
-            mm(("S1", c2, c2 + 2), ("HH", 128 * j, 128 * j + 128), ("RR", 2 * j, 2 * j + 2), group=("m", t))
-        ts(("KK", 0, 128), E, cTR, Op.is_ge, 2 * BIG, Op.mult)
-        tt(("FF", 0, 128), ("KK", 0, 128), ("CH", 0, 128), Op.subtract)
-        ts(cMM, col("S1", c2), col("S1", c2 + 1), Op.add, cINV, Op.add)
-        ts(("RW", 0, 8), ("MA", 0, 8), cMM, Op.mult)
-        mm(("S1", c3, c3 + 8), ("BM", 0, 128), ("RW", 0, 8))
-        MO, CO = ("MO", 0, 8), ("CO", 0, 8)
-        cp(MO, ("S1", c3, c3 + 8))
+            mm(("S", c2, c2 + 2), blk("HH", j), ("RR", 2 * j, 2 * j + 2), group=("m", t))
+        mm(("S", c2, c2 + 2), blk("IDH", 0), ("IV", 0, 2), group=("m", t))
+        MO, MU, CO = ("MO", 0, 8), ("MO", 8, 16), ("CO", 0, 8)
+        ts(("RW", 8, 16), ("MA", 0, 8), col("S", c2 + 1), Op.mult)
+        ts(("RW", 0, 8), ("MA", 0, 8), col("S", c2), Op.mult)
+        mm(("S", c3, c3 + 16), ("BM", 0, 128), ("RW", 0, 16))
+        cp(("MO", 0, 16), ("S", c3, c3 + 16))
         XM = ("XM", 0, 128)
-        ts(XM, ("ind", (XN, G, NP), MO), 0.5, Op.mult)
+        scale("x", XM, ("ind", (XN, G, G + NONE + 8), MU) if early else ("ind", (XN, G, NP), MO), 0.5)
         cp(("ind", (XN, G, NP), MO), XM)
-        if not last:
+        nxt = [] if last else chunks(t + 1, cfg)
+        if last:
+            dma("S", ("yx", 0, L0), (XN, G, G + L0), "st0")
+        elif not early:
             send(t + 1, XN)
-            for c in range(2):
-                xcopy(XN, c, B)
-        else:
-            dma("S", ("yx", 0, L0), (XN, G, G + L0), "st0", 128 * L0 * 4)
         if t:
             cp(("ind", (XN, G + L0, NP), CO), XM)
         else:
             cp((XN, G + L0, G + L0 + CAP), XM)
+        if last:
+            dma("S", ("yx", L0, LM), (XN, G + L0, NP), "st1")
+        for ch in nxt:
+            xcopy(t + 1, XN, *ch[:3])
+        scale("g", ("GG", 0, 128), ("ind", ("PL", 0, NONE + 8), MU), col("NR", t))
+        todo = list(nxt)
         if not last:
-            xcopy(XN, 2, width(t + 1, 2))
-        else:
-            dma("S", ("yx", L0, LM), (XN, G + L0, NP), "st1", 128 * (LM - L0) * 4)
-        Lw = ("L", LP, LP + LM)
-        tt(("LA", 0, 128), ("ind", Lw, MO), ("FF", 0, 128), Op.min)
-        cp(("ind", Lw, MO), ("LA", 0, 128))
-        tt(("GG", 0, 128), ("ind", ("PL", 0, LM), MO), ("KK", 0, 128), Op.add)
-        for c in chunks:
-            w = width(t, c)
-            o0 = B * c
-            tt((WN, G + o0, G + o0 + w), ("L", LP + o0, LP + o0 + w), ("VL%d" % c, 0, w), Op.min)
-            act(("L", LP + o0, LP + o0 + w), (WN, G + o0, G + o0 + w), Fn.Abs)
-        if not last:
-            offsets(0, B)
-            offsets(1, B)
-        else:
-            dma("A", ("yn", 0, L0), ("L", LP, LP + L0), "st2", 128 * L0 * 4)
-        LC = ("LC", 0, 128)
-        tt(LC, ("ind", Lw, MO), ("GG", 0, 128), Op.min)
-        if t:
-            cp(("ind", ("L", LP + L0, LP + LM), CO), LC)
-        else:
-            cp(("L", LP + L0, LP + L0 + CAP), LC)
-        if not last:
-            offsets(2, width(t + 1, 2))
-            w = width(t + 1, 2)
-            dma("S", (WN, G + L0, G + L0 + w), ("L", LP + L0, LP + L0 + w), "wt%d" % t, 128 * w * 4)
-        else:
-            dma("A", ("yn", L0, LM), ("L", LP + L0, LP + LM), "st3", 128 * (LM - L0) * 4)
+            ts(("V2", 8, 8 + ne), ("S", c1, c1 + ne), CAP + 1.0 - SHIFT, Op.min, cNH, Op.add)
+            for a in range(8):
+                for h in range(2):
+                    mm(("S", CM + a, CM + 8 * ne, 8), blk("BA", a), ("V2", 8 * h, 8 * h + ne), group=("cm", t, a))
+        for c, o0, w, how in chs:
+            i = INST.index((t, c))
+            A = w // 16
+            kd, ks = split(t, c)
+            VL, gr = (vl(t, c), 0, w), ("vl", i)
+            for k in range(15, -1, -1) if c >= 2 and VL[0] in ("VL0", "VL1") else ():
+                mm(VL, ("YB", 15 - k, 143 - k), ("C", cat[c, k], cat[c, k] + w), group=gr)
+            at = {}
+            if natural(t, c):
+                q0 = take("QS", 16 * w)
+                for v0 in range(0, w, 128):
+                    if v0 >= w - cfg["NV"]:
+                        for h in range(v0, v0 + 128, 32):
+                            cp(("QS", q0 + 16 * h, q0 + 16 * h + 512), ("ind", (W, 0, top), ("OT1", h, h + 32)))
+                        continue
+                    j = act(("QS", q0 + 16 * v0, q0 + 16 * v0 + 2048), ("ind", (W, 0, top), ("OT1", v0, v0 + 128)), Fn.Copy)
+                    ops[j]["soft"] = prevq[-1:]
+                    prevq.append(j)
+                for k in range(16):
+                    mm(VL, blk("ND", k), ("QS", q0 + k, q0 + 16 * w, 16), group=gr)
+                kd = ks = 0
+            for k0, k1 in kcalls(0, ks, cfg["KQ"]):
+                q0 = take("QS", (k1 - k0) * w)
+                j = act(("QS", q0, q0 + (k1 - k0) * w), ("ind", (W, 0, top), (OT, o0 + k0 * A, o0 + k1 * A)), Fn.Copy)
+                ops[j]["soft"] = prevq[-1:]
+                prevq.append(j)
+                for k in range(k0, k1):
+                    at[k] = ("QS", q0 + (k - k0) * w, q0 + (k - k0 + 1) * w)
+                    if k < kd:
+                        j = dma("S", ("QD", o0, o0 + w), at[k], "dq%d" % i, group=("dq", i), rows=k)
+                        ops[j]["lat"] += cfg["dp0"] if c == 0 else 0.0
+                    else:
+                        mm(VL, blk("ND", k), at[k], group=gr)
+            for k0, k1 in kcalls(ks, 16, cfg["KW"]) if not natural(t, c) else ():
+                q0 = take("QH", (k1 - k0) * w)
+                cp(("QH", q0, q0 + (k1 - k0) * w), ("ind", (W, 0, top), (OT, o0 + k0 * A, o0 + k1 * A)))
+                for k in range(k0, k1):
+                    mm(VL, blk("NH", k - 8), ("QH", q0 + (k - k0) * w, q0 + (k - k0 + 1) * w), group=gr)
+            if kd:
+                mm(VL, blk("NI", kds.index(kd)), ("QD", o0, o0 + w), group=gr)
+            EN = ("T3", o0, o0 + w)
+            tt(EN, (W, G + o0, G + o0 + w), VL, Op.min)
+            act((WN, G + o0, G + o0 + w), EN, Fn.Abs)
+            while todo and todo[0][1] + todo[0][2] <= min(o0 + w, L0):
+                ch = todo.pop(0)
+                offsets(t + 1, WN, ch[1], ch[2], VL[0], True)
+        LA = ("LA", 0, 128)
+        scale("l", LA, ("ind", (WN, G, NP), MO), col("NR", 4 + t))
+        tt(("ind", (WN, G, NP), MO), LA, ("CH", 0, 128), Op.add)
+        if last:
+            dma("S", ("yn", 0, L0), (WN, G, G + L0), "st3")
+        tt(("ind", (WN, G + L0, NP), CO) if t else (WN, G + L0, G + L0 + CAP), LA, ("GG", 0, 128), Op.add)
+        for j, ch in enumerate(todo):
+            offsets(t + 1, WN, ch[1], ch[2], "VL%d" % ((i + j) % 2))
+        if last:
+            dma("A", ("yn", L0, LM), (WN, G + L0, NP), "st2")
     return ops
 
 
-def schedule(ops, cfg=None):
-    cfg = cfg or CFG
+def schedule(ops, cfg=CFG):
+    if cfg.get("sets"):
+        return arrange2(cfg)
+    if cfg.get("turns"):
+        return arrange(ops, cfg)
     n = len(ops)
     succ = [[] for _ in range(n)]
     for o in ops:
@@ -453,11 +626,13 @@ def schedule(ops, cfg=None):
             succ[d].append(o["id"])
 
     def span(o):
-        return o["cost"] + (o["lat"] + o["nbytes"] / cfg["bw"] if "nbytes" in o else 0.0)
+        return o["cost"] + (o["lat"] + o["busy"] if "busy" in o else 0.0)
 
     prio = [0.0] * n
     for o in reversed(ops):
-        prio[o["id"]] = span(o) + cfg["sem"] + max([prio[s] for s in succ[o["id"]]], default=0.0)
+        prio[o["id"]] = max(prio[o["id"]], span(o) + cfg["sem"] + max([prio[s] for s in succ[o["id"]]], default=0.0))
+        for j in o.get("soft", ()) if "CH" in cfg else ():
+            prio[j] = max(prio[j], prio[o["id"]] + ops[j]["cost"])
     left = [len(o["deps"]) for o in ops]
     ready_at = [0.0] * n
     done = [0.0] * n
@@ -501,19 +676,223 @@ def schedule(ops, cfg=None):
         o = ops[i]
         start[i] = tm
         free[e] = tm + o["cost"]
-        if "nbytes" in o:
+        if "busy" in o:
             extra = 0.0
             if e == "G" and state["first"]:
                 state["first"] = False
                 extra = cfg["first"]
             s0 = max(free[e] + o["lat"] / 2 + extra, state["dma"])
-            state["dma"] = s0 + o["nbytes"] / cfg["bw"]
+            state["dma"] = s0 + o["busy"]
             done[i] = state["dma"] + o["lat"] / 2
         else:
             done[i] = free[e]
         order[e].append(i)
         release(i)
     return order, start, done
+
+
+lam = [1e9]
+
+
+def sweep(nodes, before, after, prio, look):
+    n = len(nodes)
+    left = [len(b) for b in before]
+    ready = [0.0] * n
+    start = [0.0] * n
+    pool = {e: [] for e in "VAPGSD"}
+    free = {e: 0.0 for e in pool}
+    order = {e: [] for e in pool}
+    todo = [i for i in range(n) if not left[i]]
+
+    def settle():
+        while todo:
+            i = todo.pop()
+            if nodes[i][0] == "X":
+                finish(i, ready[i])
+            else:
+                pool[nodes[i][0]].append(i)
+
+    def finish(i, tm):
+        start[i] = tm
+        for s, delay in after[i]:
+            ready[s] = max(ready[s], tm + nodes[i][1] + delay)
+            left[s] -= 1
+            if not left[s]:
+                todo.append(s)
+
+    settle()
+    while True:
+        best = None
+        for e in pool:
+            if pool[e]:
+                tm = max(free[e], min(ready[i] for i in pool[e]))
+                if best is None or tm < best[0]:
+                    best = (tm, e)
+        if best is None:
+            return order, start
+        tm, e = best
+        if e == "D" and look is not None:
+            i = min(pool[e], key=lambda j: ready[j])
+        else:
+            i = max((i for i in pool[e] if ready[i] <= tm), key=lambda j: (prio[j], -j))
+            soon = [j for j in pool[e] if tm < ready[j] < tm + nodes[i][1] and prio[j] > prio[i]]
+            if soon and look != 0.0:
+                j = max(soon, key=lambda j: prio[j])
+                wait = ready[j] - tm
+                if max(wait + prio[j], wait + nodes[j][1] + prio[i]) + abs(look or lam[0]) * wait < max(prio[i], nodes[i][1] + prio[j]):
+                    i = j
+        tm = max(tm, ready[i])
+        pool[e].remove(i)
+        free[e] = tm + nodes[i][1]
+        order[e].append(i)
+        finish(i, tm)
+        settle()
+
+
+def arrange(ops, cfg=CFG):
+    n = len(ops)
+    nodes = [(o["eng"], o["cost"]) for o in ops]
+    tail = {}
+    edges = []
+    first = True
+    for o in ops:
+        if "busy" in o:
+            tail[o["id"]] = len(nodes)
+            nodes.append(("D", o["busy"]))
+            edges.append((o["id"], tail[o["id"]], o["lat"] / 2 + (cfg["first"] if first and o["eng"] == "G" else 0.0)))
+            first = first and o["eng"] != "G"
+    for o in ops:
+        for d in o["deps"]:
+            if d in tail:
+                edges.append((tail[d], o["id"], ops[d]["lat"] / 2 + cfg["sem"]))
+            else:
+                edges.append((d, o["id"], cfg["sem"]))
+        for d in o.get("soft", ()):
+            edges.append((d, o["id"], 0.0))
+    m = len(nodes)
+    before, after = [[] for _ in range(m)], [[] for _ in range(m)]
+    for a, b, delay in edges:
+        after[a].append((b, delay))
+        before[b].append((a, delay))
+    prio = [-float(i) for i in range(n)] + [0.0] * (m - n)
+    best = None
+    for turn in range(cfg["turns"]):
+        order, start = sweep(nodes, before, after, prio, cfg["look"])
+        done = [start[i] + nodes[i][1] for i in range(m)]
+        if best is None or max(done) < best[0] or cfg["keep"]:
+            best = (max(done), order, start, done)
+        if "all" in cfg:
+            cfg["all"].append({e: order[e] for e in "VAPGS"})
+        back = sweep(nodes, after, before, done, None)[1]
+        prio = [back[i] + nodes[i][1] for i in range(m)]
+    end, order, start, done = best
+    for i in tail:
+        done[i] = done[tail[i]] + ops[i]["lat"] / 2
+    return {e: order[e] for e in "VAPGS"}, start[:n], done[:n]
+
+
+def sweep2(eng, cost, before, after, prio, look, fifo):
+    n, k = cost.shape
+    left = [len(b) for b in before]
+    ready = np.zeros((n, k))
+    start = np.zeros((n, k))
+    mean = [0.0] * n
+    pool = {e: [] for e in "VAPGSD"}
+    free = {e: np.zeros(k) for e in pool}
+    fmean = {e: 0.0 for e in pool}
+    order = {e: [] for e in pool}
+    todo = [i for i in range(n) if not left[i]]
+
+    def finish(i, tm):
+        start[i] = tm
+        end = tm + cost[i]
+        for s, delay in after[i]:
+            np.maximum(ready[s], end + delay, out=ready[s])
+            left[s] -= 1
+            if not left[s]:
+                todo.append(s)
+
+    def settle():
+        while todo:
+            i = todo.pop()
+            if eng[i] == "X":
+                finish(i, ready[i])
+            else:
+                mean[i] = float(ready[i].mean())
+                pool[eng[i]].append(i)
+
+    settle()
+    while True:
+        best = None
+        for e in pool:
+            if pool[e]:
+                tm = max(fmean[e], min(mean[i] for i in pool[e]))
+                if best is None or tm < best[0]:
+                    best = (tm, e)
+        if best is None:
+            return order, start
+        tm, e = best
+        can = pool[e]
+        if len(can) == 1:
+            i = can[0]
+        elif e == "D" and fifo:
+            i = min(can, key=lambda j: mean[j])
+        else:
+            wait = np.maximum(ready[can] - free[e], 0.0).mean(axis=1)
+            i = max(zip(can, wait), key=lambda x: (prio[x[0]] - look * x[1], -x[0]))[0]
+        tm = np.maximum(free[e], ready[i])
+        can.remove(i)
+        free[e] = tm + cost[i]
+        fmean[e] = float(free[e].mean())
+        order[e].append(i)
+        finish(i, tm)
+        settle()
+
+
+def arrange2(cfg=CFG):
+    sets = [dict(cfg, **s) for s in cfg["sets"]]
+    built = [build(s) for s in sets]
+    ops = built[0]
+    n = len(ops)
+    unit = np.array([1.0 / max(sum(o["cost"] for o in b if o["eng"] == e) for e in "VA") for b in built]) * 180000.0
+    eng = [o["eng"] for o in ops]
+    cost = [[b[i]["cost"] for b in built] for i in range(n)]
+    sem = np.array([s["sem"] for s in sets]) * unit
+    tail, lat, edges, first = {}, {}, [], True
+    for o in ops:
+        if "busy" in o:
+            i = o["id"]
+            tail[i] = len(eng)
+            eng.append("D")
+            cost.append([b[i]["busy"] for b in built])
+            lat[i] = np.array([b[i]["lat"] / 2 for b in built]) * unit
+            extra = np.array([s["first"] for s in sets]) * unit if first and o["eng"] == "G" else 0.0
+            edges.append((i, tail[i], lat[i] + extra))
+            first = first and o["eng"] != "G"
+    for o in ops:
+        for d in o["deps"]:
+            edges.append((tail[d], o["id"], lat[d] + sem) if d in tail else (d, o["id"], sem))
+        for d in o.get("soft", ()):
+            edges.append((d, o["id"], 0.0))
+    cost = np.array(cost) * unit
+    m = len(eng)
+    before, after = [[] for _ in range(m)], [[] for _ in range(m)]
+    for a, b, delay in edges:
+        after[a].append((b, delay))
+        before[b].append((a, delay))
+    prio = [-float(i) for i in range(n)] + [0.0] * (m - n)
+    best = None
+    for turn in range(cfg["turns"]):
+        order, start = sweep2(eng, cost, before, after, prio, cfg["look"], True)
+        done = start + cost
+        ends = done.max(axis=0)
+        mark = float(ends.mean() + 0.5 * ends.max())
+        if best is None or mark < best[0]:
+            best = (mark, order, start.mean(axis=1), done.mean(axis=1))
+        back = sweep2(eng, cost, after, before, list(done.mean(axis=1)), cfg["look"], False)[1]
+        prio = list((back + cost).mean(axis=1))
+    mark, order, start, done = best
+    return {e: order[e] for e in "VAPGS"}, list(start[:n]), list(done[:n])
 
 
 PLAN = []
@@ -531,11 +910,11 @@ def helper_program(g, core, owner, T, topo):
     rid, pid, _ = topo.addr(owner)
     m = topo.mask(core, owner)
     sent = 0
-    for i, (t, c) in enumerate(INST):
-        if fold_units(t, c):
-            lo, hi = fold_cols(t, c)
+    for o in plan()[0]:
+        if o["kind"] == "fold":
+            i, o0, w = o["args"]
             g.wait_ge(T.sem["ha%d" % i], 16)
-            g.remote_dma(T.YZ[:, lo:hi], T.YZ[:, lo:hi], T.sem["ya%d" % i], T.sem.hback, pid, rid, m)
+            g.remote_dma(T.Y[:, o0:o0 + w], T.Y[:, o0:o0 + w], T.sem["ya%d" % i], T.sem.hback, pid, rid, m)
             sent += len(topo.engines(core, owner))
     g.wait_ge(T.sem.hback, sent)
 
@@ -594,6 +973,8 @@ def rank_program(g, core, T, topo):
             if SCRATCH[a[0][0]][2] == "int32":
                 return q.iota(ap(a[0]), a[1], a[2], a[3])
             return q.iota(ap(a[0]), a[1], a[2], a[3], allow_small_or_imprecise_dtypes=True)
+        if kind == "select":
+            return q.affine_select(ap(a[0]), ap(a[1]), *a[2:])
         if kind == "dma":
             if a[2] is None:
                 return q.dma_start(ap(a[0]), ap(a[1]))
@@ -611,19 +992,11 @@ def rank_program(g, core, T, topo):
             g.remote_dma_fused(trs, local_sem=T.sem[o["sem"]])
             return None
         if kind == "fold":
-            i, t, c = a
-            w = width(t, c)
-            us = fold_units(t, c)
+            i, o0, w = a
             rid, pid, _ = topo.addr(helper)
-            en = topo.engines(core, helper)
-            trs = []
-            for j, u in enumerate(us):
-                part = en[j * len(en) // len(us):(j + 1) * len(en) // len(us)]
-                lo = 2 * B * c + (0 if u == "y" else w)
-                trs.append(RemoteDMATransfer(dst_ids=[DstId(rid=rid, pnc=pid)], dma_engine_mask=mask_of(part), remote_sem=T.sem["ha%d" % i],
-                                             srcs=[T["P%d" % c][:, k * w:k * w + w] for k in range(16)], dsts=[T.YZ[:, lo:lo + w]],
-                                             alu_op=2 if u == "y" else 3))
-            g.remote_dma_fused(trs, local_sem=T.sem[o["sem"]])
+            tr = RemoteDMATransfer(dst_ids=[DstId(rid=rid, pnc=pid)], dma_engine_mask=topo.mask(core, helper), remote_sem=T.sem["ha%d" % i],
+                                   srcs=[T.P[:, 16 * o0 + k * w:16 * o0 + k * w + w] for k in range(16)], dsts=[T.Y[:, o0:o0 + w]], alu_op=2)
+            g.remote_dma_fused([tr], local_sem=T.sem[o["sem"]])
             return None
         out, ins, x = a
         if kind == "ts":
@@ -637,10 +1010,12 @@ def rank_program(g, core, T, topo):
         if kind == "tr":
             return q.transpose(ap(out), ap(ins[0]))
         if kind == "scan":
-            return q.tensor_tensor_scan(ap(out), ap(ins[0]), ap(ins[1]), 0.0, Op.mult, Op.add)
-        if x[1] is None:
-            return q.activation(ap(out), ap(ins[0]), x[0])
-        return q.activation(ap(out), ap(ins[0]), x[0], scale=x[1])
+            return q.tensor_tensor_scan(ap(out), ap(ins[0]), ap(ins[1]), ap(ins[2]), Op.mult, Op.add)
+        if ins[1] is not None:
+            return q.activation(ap(out), ap(ins[0]), x, bias=ap(ins[1]), scale=ap(ins[2]))
+        if ins[2] is None:
+            return q.activation(ap(out), ap(ins[0]), x)
+        return q.activation(ap(out), ap(ins[0]), x, scale=ap(ins[2]))
 
     for e in "SAVPG":
         q = queue[e]
@@ -649,8 +1024,9 @@ def rank_program(g, core, T, topo):
             o = ops[i]
             want = {}
             for d in o["deps"]:
-                s, v = event[d]
-                want[s] = max(want.get(s, 0), v)
+                if d in event:
+                    s, v = event[d]
+                    want[s] = max(want.get(s, 0), v)
             for s, v in sorted(want.items()):
                 if known.get(s, 0) < v:
                     q.wait_ge(T.sem[s], v)

import numpy as np
from concourse.bass import DstId, RemoteDMATransfer
from concourse.mybir import AluOpType, ActivationFunctionType

N = 4
L0, CAP, RO, B, OFF, H = 768, 128, 4, 384, (3, 1), 72
G = B * len(OFF)
LM = L0 + RO * CAP
LW = LM - CAP
NP = G + LM
VOID = NP - 1
NONE = LM + B
BIG = 4096.0
SHIFT = 1281.0
WM = 512
QS_N, QH_N = 11520, 3072
CM = 64

CFG = {
    "CH": [[(384, "f"), (384, "f")],
           [(384, "f"), (384, "f"), (128, "f")],
           [(384, "f"), (384, "f"), (256, "f")],
           [(384, "f"), (384, "f"), (384, "f")]],
    "KV": [[4, 0], [4, 0, 0], [4, 0, 0], [4, 0, 0]],
    "QV": [[0, 0], [0, 0, 0], [0, 0, 0], [0, 0, 4]],
    "QP": [[0, 0], [2, 0, 0], [0, 0, 0], [0, 0, 4]],
    "TV": 2,
    "KC": 4, "KQ": 3, "KW": 1,
    "EG": True,
    "ST": [768],
    "dp0": 2000.0, "keep": False, "OV": [], "B3": {}, "NV": 128, "pad": [0.0, 0.0, 0.0, 0.0], "dpad": 0.0, "P75": True, "ZP": True, "NAT": True, "SA": "", "look": 0.0, "turns": 5,
    "f": 1.15, "gath": 1.48, "scat": 3.2, "bw": 472.0, "row": 6.0, "fix": 15.0, "pfix": 30.0, "sem": 100.0, "rlat": 2600.0,
    "riss": 600.0, "dlat": 1600.0, "diss": 120.0, "first": 2500.0, "gf": 1.08,
}


def chunks(t, cfg=CFG):
    out, o0 = [], 0
    for c, (w, how) in enumerate(cfg["CH"][t]):
        out.append((c, o0, w, how))
        o0 += w
    return out


def instances(cfg=CFG):
    return [(t, c) for t in range(RO) for c in range(len(cfg["CH"][t]))]


F32, BF, F16 = "float32", "bfloat16", "float16"
SCRATCH = {
    "X0": ("sbuf", [128, G + NONE + 8], F32), "X1": ("sbuf", [128, G + NONE + 8], F32),
    "FC": ("sbuf", [128, 8], F32), "DG": ("sbuf", [128, B], BF), "IDB": ("sbuf", [128, 128], BF),
    "W0": ("sbuf", [128, NP], F32), "W1": ("sbuf", [128, NP], F32),
    "NB": ("sbuf", [128, L0], "int32"),
    "OF": ("sbuf", [128, 48], F32), "OG": ("sbuf", [128, 48], F32), "BA": ("sbuf", [128, 8 * 128], F16),
    "V1": ("sbuf", [128, 8], F32), "V2": ("sbuf", [128, 16], F16), "NR": ("sbuf", [128, 8], F32),
    "P": ("sbuf", [128, 16 * LW], F32), "C": ("sbuf", [128, 24 * B], BF),
    "QS": ("sbuf", [128, QS_N], F32), "QH": ("sbuf", [128, QH_N], F16), "QD": ("sbuf", [128, LW], F32),
    "Y": ("sbuf", [128, LW], F32), "T3": ("sbuf", [128, LW], F32), "BV": ("sbuf", [128, LW], BF),
    "T1": ("sbuf", [128, 2 * WM], F16),
    "OT0": ("sbuf", [128, LW], "uint16"), "OT1": ("sbuf", [128, LW], "uint16"),
    "PL": ("sbuf", [128, NONE + 8], F32),
    "IM": ("sbuf", [128, 144], F32), "IB": ("sbuf", [128, 240], BF), "I16": ("sbuf", [128, 128], BF),
    "PI": ("sbuf", [128, 8], "int32"), "CF": ("sbuf", [128, 16], F32), "NM": ("sbuf", [128, 16], F32),
    "CG": ("sbuf", [128, 8], F32), "I2": ("sbuf", [128, 24], F32), "LS": ("sbuf", [128, 48], "uint16"),
    "ZC": ("sbuf", [128, 8], F32), "ZZ": ("sbuf", [128, 9 * 128], F16), "R32": ("sbuf", [128, 24], F32),
    "YB": ("sbuf", [128, 144], BF), "ID": ("sbuf", [128, 128], F32), "IQ": ("sbuf", [128, 128], F32), "IN": ("sbuf", [128, 128], F32),
    "NI": ("sbuf", [128, 4 * 128], F32), "ND": ("sbuf", [128, 16 * 128], F32), "NH": ("sbuf", [128, 8 * 128], F16),
    "TRI": ("sbuf", [128, 128], BF), "ONE": ("sbuf", [128, 128], BF), "HALF": ("sbuf", [128, 8], BF), "E1": ("sbuf", [128, 128], F16),
    "BM": ("sbuf", [128, 128], F16), "MA": ("sbuf", [128, 8], F32), "WE": ("sbuf", [128, 8], F32),
    "RR": ("sbuf", [128, 24], F16), "P2": ("sbuf", [128, 8], F32), "IV": ("sbuf", [128, 8], F16), "IDH": ("sbuf", [128, 128], F16),
    "RB": ("sbuf", [128, 16], BF), "RS": ("sbuf", [128, 16], BF), "CR": ("sbuf", [128, 16], F32),
    "HH": ("sbuf", [128, 9 * 128], F16),
    "ST": ("sbuf", [128, 32], F32), "RW": ("sbuf", [128, 16], F16),
    "MO": ("sbuf", [128, 16], "uint16"), "CO": ("sbuf", [128, 8], "uint16"),
    "CH": ("sbuf", [128, 128], F32), "GG": ("sbuf", [128, 128], F32), "XM": ("sbuf", [128, 128], F32), "LA": ("sbuf", [128, 128], F32),
    "XP0": ("psum", [128, 512], F32), "XP1": ("psum", [128, 512], F32), "XP2": ("psum", [128, 512], F32),
    "VL0": ("psum", [128, 512], F32), "VL1": ("psum", [128, 512], F32),
    "Z": ("psum", [128, 512], F32), "A": ("psum", [128, 512], F32), "S": ("psum", [128, 512], F32),
}

SEMAPHORES = (["eV", "eA", "eP", "eG", "hback"] + ["ld%d" % i for i in range(4)] + ["st%d" % i for i in range(8)]
              + ["cp%d" % i for i in range(8)] + ["lc%d" % i for i in range(RO)]
              + ["gl%d" % i for i in range(RO)] + ["ga%d" % i for i in range(RO)] + ["gb%d" % i for i in range(RO)]
              + ["%s%d" % (s, i) for s in ("fl", "ha", "ya", "dq") for i in range(len(instances()))])

ESEM = {"V": "eV", "A": "eA", "P": "eP", "G": "eG"}
Op = AluOpType
Fn = ActivationFunctionType


def helper_of(core, T, topo):
    mates = [c for c in topo.cores_of(core) if topo.die(c) == topo.die(core)]
    ranks = [c for c in mates if T.rank_of(c) is not None]
    free = [c for c in mates if T.rank_of(c) is None]
    return free[ranks.index(core) % len(free)]


def mask_of(engines):
    m = 0
    for e in engines:
        m |= 1 << e
    return m


def meet(r, s):
    if r[1] >= s[2] or s[1] >= r[2]:
        return False
    if len(r) > 3 and len(s) > 3 and r[3] == s[3]:
        return (r[1] - s[1]) % r[3] == 0
    return True


def build(cfg=CFG):
    ops = []
    hist = {}
    bysem = {}
    inbank = {}
    late = []
    cyc = 0.83 * cfg["f"]
    gcyc = 0.83 * cfg["gf"]
    INST = instances(cfg)

    def psum(name):
        return name in SCRATCH and SCRATCH[name][0] == "psum"

    def regs(a):
        if a[0] == "ind":
            return [a[1], a[2]]
        return [a]

    def add(eng, kind, args, reads, writes, cost, group=None, after=(), **kw):
        o = dict(id=len(ops), eng=eng, kind=kind, args=args, cost=cost, group=group, deps=set(after), **kw)
        acc = [(r, False) for r in reads] + [(r, True) for r in writes]
        for r, wr in acc:
            for (s, oid, ow, oe, og) in hist.get(r[0], []):
                if group is not None and og == group and wr and ow:
                    continue
                if psum(r[0]) and oe != eng:
                    o["deps"].add(oid)
                elif (wr or ow) and meet(r, s):
                    o["deps"].add(oid)
        for d in list(o["deps"]):
            if "sem" in ops[d]:
                o["deps"].update(bysem[ops[d]["sem"]])
        if "sem" in o:
            bysem.setdefault(o["sem"], []).append(o["id"])
        for r, wr in acc:
            h = hist.setdefault(r[0], [])
            if wr and group is None and len(r) == 3 and not psum(r[0]) and not kw.get("part"):
                h[:] = [x for x in h if not (r[1] <= x[0][1] and x[0][2] <= r[2])]
            if psum(r[0]) and h and h[-1][3] != eng:
                j = len(h)
                while j and h[j - 1][3] != eng:
                    j -= 1
                del h[:j]
            h.append((r, o["id"], wr, eng, group))
        ops.append(o)
        return o["id"]

    def nel(a):
        if a[0] == "ind":
            return 16 * (a[2][2] - a[2][1])
        return len(range(a[1], a[2], a[3] if len(a) > 3 else 1))

    def two(a):
        return SCRATCH[a[0]][2] in (BF, F16, "uint16")

    def comp(eng, kind, out, ins, args, mult=1.0):
        reads, writes = [], []
        for a in ins:
            if isinstance(a, tuple):
                reads += regs(a)
        part = False
        if out[0] == "ind":
            writes.append(out[1]); reads.append(out[2]); part = True
            cost = 50 + nel(out) * cfg["scat"] * gcyc
        else:
            writes.append(out)
            if isinstance(ins[0], tuple) and ins[0][0] == "ind":
                cost = (50 if eng == "V" else 65) + nel(out) * cfg["gath"] * gcyc
            else:
                cost = cfg["fix"] + max(64, nel(out) * mult) * cyc
        return add(eng, kind, (out, ins, args), reads, writes, cost, part=part)

    def ts(out, a, s1, op0, s2=None, op1=None):
        half = a[0] != "ind" and out[0] != "ind" and two(a) and two(out)
        return comp("V", "ts", out, [a, s1, s2], (op0, op1), 0.5 if half else 1.0)

    def tt(out, a, b, op):
        both = a[0] != "ind" and not psum(a[0]) and not psum(b[0])
        return comp("V", "tt", out, [a, b], op, 2.0 if both else 1.0)

    def cp(out, a):
        return comp("V", "cp", out, [a], None)

    def act(out, a, fn, scale=None, bias=None):
        return comp("A", "act", out, [a, bias, scale], fn)

    def scale(tag, out, a, s):
        return act(out, a, Fn.Copy, s) if tag in cfg["SA"] else ts(out, a, s, Op.mult)

    def mm(out, lhs, rhs, group=None, behind=()):
        k = 4 if SCRATCH[rhs[0]][2] == F32 else 1
        prev = inbank.setdefault(out[0], [])
        soft = [j for j in prev if group is None or ops[j]["group"] != group] + list(behind)
        j = add("P", "mm", (out, lhs, rhs), [lhs, rhs], [out], cfg["pfix"] + max(64, nel(rhs)) * k * cyc / 2, group=group, soft=soft)
        prev[:] = prev[-40:] + [j]
        return j

    def iota(out, pattern, base, cm=0):
        return add("G", "iota", (out, pattern, base, cm), [], [out], 130 + 2 * nel(out) * cyc, soft=list(late))

    def select(out, a, pattern, op, val, base, cm):
        return add("G", "select", (out, a, pattern, op, val, base, cm), [a], [out], 170 + 2 * nel(out) * cyc, soft=list(late))

    def fill(out, val):
        return iota(out, [[0, nel(out)]], val)

    def dma(eng, out, a, sem, group=None, rows=None):
        n = 128 if rows is None else 8
        return add(eng, "dma", (out, a, rows), [a], [out], cfg["diss"], group=group, sem=sem, inc=16, lat=cfg["dlat"] + (cfg["dpad"] if rows is not None else 0.0),
                   busy=n * nel(a) * 4 / cfg["bw"] + max(n, 16) * cfg["row"] / 16, part=rows is not None)

    def send(t, buf):
        s = add("G", "send", (buf, t), [(buf, G, G + B)], [], cfg["riss"], sem="gl%d" % t, inc=16, lat=cfg["rlat"],
                busy=2 * 128 * B * 4 / cfg["bw"] + 16 * cfg["row"])
        if t == 0:
            late.append(s)
        for d in range(2):
            add("X", "arrive", None, [], [(buf, d * B, d * B + B)], 300.0, after=[s], sem=("ga%d", "gb%d")[d] % t, inc=8)
        return s

    def col(name, j):
        return (name, j, j + 1)

    def blk(name, j):
        return (name, 128 * j, 128 * j + 128)

    E = ("IM", 15, 143)
    ID, IQ, IN = blk("ID", 0), blk("IQ", 0), blk("IN", 0)

    def esl(n):
        return ("IM", 15, 15 + n)

    cP, cB, cG, cND, cB113 = [col("CF", j) for j in range(5)]
    cVB = col("P2", 4)

    def split(t, c):
        ks = 16 - cfg["QV"][t][c]
        return ks - cfg["QP"][t][c], ks

    def natural(t, c):
        return cfg["NAT"] and t == 0 and c == 0

    rest = [(t, c) for t, c in INST if not natural(t, c)]
    kds = sorted(set(split(t, c)[0] for t, c in rest) - {0})
    nds = list(range(16)) if cfg["NAT"] else sorted(set(k for t, c in rest for k in range(*split(t, c))))
    nhs = sorted(set(k for t, c in rest for k in range(split(t, c)[1], 16)))

    dma("A", ("NB", 0, B), ("nb", 0, B), "ld1")
    dma("S", ("X0", G, G + B), ("x0", 0, B), "ld0")
    dma("A", ("NB", B, L0), ("nb", B, L0), "ld2")
    dma("S", ("X0", G + B, G + L0), ("x0", B, L0), "ld3")
    iota(("PI", 0, 1), [[0, 1]], 0, 1)
    iota(("IM", 0, 144), [[1, 144]], -15)
    if cfg["OV"]:
        iota(("I2", 0, 24), [[256, 3], [2, 8]], 0)
    iota(("IB", 0, 128), [[1, 128]], 0)
    for j in range(2):
        iota(("W0", B * j, B * j + B), [[1, B]], B * j)
    send(0, "X0")
    fill(("W0", G + L0, NP), VOID)
    fill(("X1", G + L0, NP), 0)
    dma("S", ("X0", G + L0, NP), ("X1", G + L0, NP), "cp0")
    for j in range(3):
        dma("S", ("QD", B * j, B * j + B), ("X1", G + L0, G + L0 + B), "cp1", group="qd")
    dma("S", ("W1", 0, G), ("W0", 0, G), "cp2")
    dma("S", ("W1", G + L0, NP), ("W0", G + L0, NP), "cp3")
    iota(("I16", 0, 128), [[0, 8], [1, 16]], 0)
    fill(("ONE", 0, 128), 1)
    fill(("RB", 0, 16), 0)
    fill(("RS", 0, 16), 0)
    fill(("ST", 0, 1), L0)
    for j in range(0, LM, 320):
        iota(("PL", j, j + 320), [[1, 320]], G + j)
    iota(("PL", LM, NONE), [[1, B]], G)
    fill(("PL", NONE, NONE + 8), VOID)
    for buf in ("X0", "X1"):
        fill((buf, G + NONE, G + NONE + 8), 0)
    p0 = col("PI", 0)
    ts(col("PI", 1), p0, 15, Op.bitwise_and)
    ts(col("PI", 2), p0, 112, Op.bitwise_and)
    cp(("CF", 0, 3), ("PI", 0, 3))
    ts(ID, E, cP, Op.is_equal)
    ts(("MA", 0, 8), esl(8), 16.0, Op.mult, cG, Op.is_equal)
    ts(cB113, cB, 113.0, Op.add)
    ts(("ZC", 0, 8), ("MA", 0, 8), cB113, Op.mult, -1.0, Op.add)
    for a in range(9):
        ts(blk("ZZ", a), ("IB", 0, 128), col("ZC", a) if a < 8 else -1.0, Op.is_equal)
    ts(("YB", 0, 144), ("IM", 0, 144), cG, Op.is_equal, BIG, Op.mult)
    ts(("NM", 0, 16), esl(16), cB, Op.is_equal, -1.0, Op.mult)
    act(IQ, ID, Fn.Copy, 0.25)
    act(IN, ID, Fn.Copy, -0.75 if cfg["P75"] else -1.0)
    for k in nds:
        act(blk("ND", k), ID, Fn.Copy, col("NM", k))
    for k in nhs:
        ts(blk("NH", k - 8), E, cP, Op.is_equal, col("NM", k), Op.mult)
    for j, kd in enumerate(kds):
        ts(col("CF", 9 + j), cB, float(kd), Op.is_lt, -1.0, Op.mult)
        scale("n", blk("NI", j), ID, col("CF", 9 + j))
    select(blk("TRI", 0), blk("ONE", 0), [[1, 128]], Op.is_ge, 0.0, 0, -1)
    select(blk("TRI", 0), blk("TRI", 0), [[1, 128]], Op.not_equal, 1.0 - SHIFT, 0, -1)
    ts(("E1", 0, 128), E, 1.0 - SHIFT, Op.add)
    ts(("BM", 0, 128), ("I16", 0, 128), cB, Op.is_equal)
    for a in range(8):
        ts(blk("BA", a), ("I16", 0, 128), cB, Op.is_equal, col("MA", a), Op.mult)
    ts(("NR", 0, RO), esl(RO), cB, Op.is_equal)
    ts(("NR", RO, 2 * RO), esl(RO), cB, Op.not_equal)
    ts(("WE", 0, 8), esl(8), 16.0, Op.mult, cB, Op.add)
    iota(("R32", 0, 6), [[128, 3], [LM, 2]], 0, 1)
    iota(("R32", 6, 18), [[128, 6], [0, 2]], B, 1)
    cp(("RR", 0, 18), ("R32", 0, 18))
    iota(col("P2", 0), [[0, 1]], 0, 1)
    fill(col("P2", 1), int(G - 1 + SHIFT - NP))
    cp(blk("IDH", 0), ID)
    if cfg["EG"]:
        act(blk("IDB", 0), ID, Fn.Copy)
    select(col("HALF", 0), col("ONE", 0), [[0, 1]], Op.is_equal, 0.5, 1, 0)
    select(cVB, col("P2", 0), [[0, 1]], Op.is_equal, -(1.5 + 2.0 ** -23), 1, 0)

    lists = {B: ("LS", 0, 24), 128: ("LS", 24, 32), 256: ("LS", 32, 48)}
    widths = set(w for t in range(RO) for c, o0, w, how in chunks(t, cfg) if (t, o0) in cfg["OV"])
    if widths:
        cPB, cE, cHB, cDF, cC1, cD8, cD24 = [col("CG", j) for j in range(7)]
        ts(col("PI", 3), p0, 1, Op.bitwise_and)
        ts(col("PI", 4), p0, 4, Op.logical_shift_right, 1, Op.bitwise_and)
        ts(col("PI", 5), p0, 3, Op.logical_shift_right, 1, Op.bitwise_and)
        cp(("CG", 0, 3), ("PI", 3, 6))
        ts(cDF, cPB, cE, Op.not_equal, float(B + 16), Op.mult)
        ts(cC1, cB, 16.0, Op.mult, cDF, Op.add)
        if B in widths:
            ts(cD24, cHB, float(1 - B), Op.mult, cC1, Op.add)
            ts(("LS", 0, 24, 3), ("I2", 0, 8), cC1, Op.add)
            ts(("LS", 1, 24, 3), ("I2", 8, 16), cD24, Op.add)
            ts(("LS", 2, 24, 3), ("I2", 16, 24), cC1, Op.add, float(1 - B), Op.add)
        if 128 in widths:
            ts(cD8, cHB, -127.0, Op.mult, cC1, Op.add)
            ts(("LS", 24, 32), ("I2", 0, 8), cD8, Op.add)
        if 256 in widths:
            ts(("LS", 32, 48), esl(16), cC1, Op.add)

    nof = [0]

    def offsets(t, W, o0, w, bank, mend=False):
        nb, A = w // 128, w // 16
        q = WM * (nof[0] % 2)
        nof[0] += 1
        OT = "OT%d" % (t % 2)
        if (t, o0) in cfg["OV"]:
            q = take("QS", B + WM)
            comp("V", "tr", ("QS", q, q + w), [(W, G + o0, G + o0 + w)], None)
            comp("V", "tr", ("QS", q + B, q + B + w + 32), [(W, G + o0 - 16, G + o0 + w + 16)], None)
            cp((OT, o0, o0 + w), ("ind", ("QS", q, q + B + w + 32), lists[w]))
        else:
            for b in range(nb):
                mm((bank, b, w, nb), (W, G + o0 + 128 * b, G + o0 + 128 * b + 128), ID)
            cp(("T1", q, q + w), (bank, 0, w))
            for a in range(8):
                for g in range(8):
                    s = 128 * a + 112 - 16 * g
                    mm((bank, a, w, 8), ("ZZ", s, s + 128), ("T1", q + 16 * nb * g, q + 16 * nb * (g + 1)), group=("ot", t, o0, a))
            cp((OT, o0, o0 + w), (bank, 0, w))
        if mend:
            k, f = t - 1, o0 // 16
            cp(("OF", f, f + A), (OT, o0 + k * A, o0 + k * A + A))
            tt(("OG", f, f + A), ("OF", f, f + A), ("S", CM + f, CM + f + A), Op.max)
            cp((OT, o0 + k * A, o0 + k * A + A), ("OG", f, f + A))

    def xp(t, c):
        bank, at = 0, 0
        for j, o0, w, how in chunks(t, cfg):
            if at + w > WM:
                bank, at = bank + 1, 0
            if j == c:
                return ("XP%d" % bank, at, at + w)
            at += w

    def vl(t, c):
        if c == 2 and t in cfg["B3"]:
            return cfg["B3"][t]
        return "XP0" if t == RO - 1 and c == 2 and xp(t, 1)[0] != "XP0" else "VL%d" % (INST.index((t, c)) % 2)

    def xcopy(t, buf, c, o0, w):
        mm(xp(t, c), ID, (buf, G + o0, G + o0 + w))

    def kcalls(lo, hi, most):
        n = hi - lo
        if n <= 0:
            return []
        m = (n + most - 1) // most
        cuts = [lo + (n * i) // m for i in range(m + 1)]
        return list(zip(cuts[:-1], cuts[1:]))

    ring = {"QS": 0, "QH": 0, "C": 0}

    def take(name, n):
        if ring[name] + n > SCRATCH[name][1][1]:
            ring[name] = 0
        ring[name] += n
        return ring[name] - n

    for c, o0, w, how in chunks(0, cfg):
        cp(("W0", G + o0, G + o0 + w), ("NB", o0, o0 + w))
        if natural(0, c):
            cp(("OT1", 0, w), ("NB", 0, w))
    for c, o0, w, how in chunks(0, cfg):
        offsets(0, "W0", o0, w, "VL%d" % (c % 2))
        xcopy(0, "X0", c, o0, w)

    prevq, folds = [], []
    for t in range(RO):
        X, XN, W, WN = "X%d" % (t % 2), "X%d" % (1 - t % 2), "W%d" % (t % 2), "W%d" % (1 - t % 2)
        OT = "OT%d" % (t % 2)
        chs = chunks(t, cfg)
        nb = (L0 + CAP * t) // 128
        cN, cNN = col("ST", t), col("ST", t + 1)
        cNPE, cNH = col("ST", 8), col("ST", 9)
        last = t == RO - 1
        top = NP if t else G + L0
        if last:
            fill((W, VOID, NP), 0)
            fill((WN, G + LW, NP), 0)
            fill(("PL", NONE, NONE + 8), 0)
        ts(("ST", 8, 10), ("P2", 0, 2), cN, Op.add)
        if t:
            ts(("CO", 0, 8), ("WE", 0, 8), cN, Op.add, float(-L0), Op.add)
        ts(("CH", 0, 128), ("PL", 0, 128), cN, Op.add, col("NR", t), Op.mult)
        early = cfg["EG"] and not last
        c1, c2, c3 = 16, 32, 48
        jb, ne = 0, L0 // 128
        cat, reads_x = {}, []
        for c, o0, w, how in chs:
            A = w // 16
            XP = xp(t, c)
            tail = c >= len(chs) - cfg["TV"]

            def sl(buf, k0, k1=None):
                return (buf, 16 * o0 + k0 * w, 16 * o0 + (k0 + 1 if k1 is None else k1) * w)

            KV = cfg["KV"][t][c]
            for k0, k1 in kcalls(16 - KV, 16, cfg["KW"])[::-1]:
                reads_x.append(cp(sl("P", k0, k1), ("ind", (X, 0, top), (OT, o0 + k0 * A, o0 + k1 * A))))
            for k0, k1 in kcalls(0, 16 - KV, cfg["KC"])[::-1]:
                reads_x.append(act(sl("P", k0, k1), ("ind", (X, 0, top), (OT, o0 + k0 * A, o0 + k1 * A)), Fn.Copy))
            Y, T3, Z, Z2, AC = ("Y", o0, o0 + w), ("T3", o0, o0 + w), ("Z", 0, w), ("Z", 256, 256 + w), ("A", 0, w)
            if how == "f":
                i = INST.index((t, c))
                f = add("G", "fold", (i, o0, w), [sl("P", 0, 16)], [Y], cfg["riss"], sem="fl%d" % i, inc=16, lat=cfg["rlat"],
                        busy=16 * 128 * w * 4 / cfg["bw"] + 128 * cfg["row"], soft=folds[-1:])
                folds.append(f)
                add("X", "arrive", None, [], [Y], cfg["riss"] + cfg["rlat"] + 128 * w * 4 / cfg["bw"] + 8 * cfg["row"] + 300 + cfg["pad"][len(chs) - 1 - c], after=[f],
                    sem="ya%d" % i, inc=16)
            if cfg["ZP"]:
                mm(Z, ID, sl("P", 15))
            if how == "v":
                mm(Z2, ID, sl("P", 15))
            for k in range(14, -1, -1):
                tt(Z, sl("P", k), Z if cfg["ZP"] or k < 14 else sl("P", 15), Op.min)
                if how == "v":
                    tt(Z2 if k else Y, sl("P", k), Z2, Op.max)
            for k in range(15, -1, -1):
                cat[c, k] = take("C", w)
                tt(("C", cat[c, k], cat[c, k] + w), sl("P", k), XP, Op.is_gt)
                if c < 2 or vl(t, c) not in ("VL0", "VL1"):
                    mm((vl(t, c), 0, w), ("YB", 15 - k, 143 - k), ("C", cat[c, k], cat[c, k] + w), group=("vl", INST.index((t, c))))
            tt(T3, (X, G + o0, G + o0 + w), Z, Op.mult)
            if cfg["P75"]:
                pass
            elif tail:
                ts(T3, T3, 0.75, Op.mult)
            else:
                act(T3, T3, Fn.Copy, 0.75)
            gr = ("x", t, c)
            j0 = mm(AC, ID, (X, G + o0, G + o0 + w), group=gr)
            j1 = mm(AC, IQ, Y, group=gr, behind=[j0])
            mm(AC, IN, T3, group=gr, behind=[j1])
            if tail:
                ts(("BV", o0, o0 + w), AC, 1.0, Op.is_gt, -0.5, Op.add)
            mid = min(max(B, o0), o0 + w) if early else o0
            for at, lo, hi in ((NP, o0, mid), (G, mid, o0 + w)):
                if lo < hi:
                    ts((XN, at + lo, at + hi), ("A", lo - o0, hi - o0), 0.0, Op.max, 2.0, Op.min)
                    if not tail:
                        act(("BV", lo, hi), (XN, at + lo, at + hi), Fn.Sign, 1.5, cVB)
            j1 = (o0 + w) // 128
            for j in range(o0 // 128, j1):
                mm(col("S", j), blk("BV", j), col("ONE" if tail else "HALF", 0))
            ghosts = early and o0 < B <= o0 + w
            if j1 < nb and not (o0 + w in cfg["ST"] or ghosts):
                continue
            je = j1 + (j1 == nb)
            ts(("RB", jb, j1), ("S", jb, j1), float(H - 64), Op.is_ge)
            comp("V", "scan", ("RS", jb + 1, j1 + 1), [("ONE", jb, j1), ("RB", jb, j1), col("RS", jb) if jb else 0.0], None)
            mm(("S", c1 + jb, c1 + je), ("TRI", 0, 128), ("RB", jb, je), group=("c", t, c))
            mm(("S", c1 + jb, c1 + je), ("ONE", 0, 128), ("RS", jb, je), group=("c", t, c))
            jv = min(j1, ne)
            if not last and jb < jv:
                ts(("V2", jb, jv), ("S", c1 + jb, c1 + jv), CAP + 0.5 - SHIFT, Op.is_lt, float(NP), Op.mult)
            if ghosts:
                ts(("FC", 0, B // 128), ("V2", 0, B // 128), -0.5 / NP, Op.mult, 1.0, Op.add)
                for j in range(B // 128):
                    scale("d", blk("DG", j), blk("IDB", 0), col("FC", j))
                    mm(blk("A", j), blk("ONE", 0), blk("DG", j))
                tt((XN, G, G + B), (XN, NP, NP + B), ("A", 0, B), Op.mult)
                sent = send(t + 1, XN)
            for j in range(jb, j1):
                ts(blk("HH", j), ("E1", 0, 128), col("S", c1 + j), Op.is_equal)
            jb = j1
        if early:
            ops[sent]["deps"].update(reads_x)
        tot = col("S", c1 + nb)
        ts(col("IV", 0), cP, tot, Op.is_ge, cNPE, Op.mult)
        ts(col("IV", 1), cP, tot, Op.is_ge, float(NONE), Op.mult)
        if not last:
            ts(cNN, tot, float(CAP), Op.min, cN, Op.add)
        for j in range(nb):
            mm(("S", c2, c2 + 2), blk("HH", j), ("RR", 2 * j, 2 * j + 2), group=("m", t))
        mm(("S", c2, c2 + 2), blk("IDH", 0), ("IV", 0, 2), group=("m", t))
        MO, MU, CO = ("MO", 0, 8), ("MO", 8, 16), ("CO", 0, 8)
        ts(("RW", 8, 16), ("MA", 0, 8), col("S", c2 + 1), Op.mult)
        ts(("RW", 0, 8), ("MA", 0, 8), col("S", c2), Op.mult)
        mm(("S", c3, c3 + 16), ("BM", 0, 128), ("RW", 0, 16))
        cp(("MO", 0, 16), ("S", c3, c3 + 16))
        XM = ("XM", 0, 128)
        scale("x", XM, ("ind", (XN, G, G + NONE + 8), MU) if early else ("ind", (XN, G, NP), MO), 0.5)
        cp(("ind", (XN, G, NP), MO), XM)
        nxt = [] if last else chunks(t + 1, cfg)
        if last:
            dma("S", ("yx", 0, L0), (XN, G, G + L0), "st0")
        elif not early:
            send(t + 1, XN)
        if t:
            cp(("ind", (XN, G + L0, NP), CO), XM)
        else:
            cp((XN, G + L0, G + L0 + CAP), XM)
        if last:
            dma("S", ("yx", L0, LM), (XN, G + L0, NP), "st1")
        for ch in nxt:
            xcopy(t + 1, XN, *ch[:3])
        scale("g", ("GG", 0, 128), ("ind", ("PL", 0, NONE + 8), MU), col("NR", t))
        todo = list(nxt)
        if not last:
            ts(("V2", 8, 8 + ne), ("S", c1, c1 + ne), CAP + 1.0 - SHIFT, Op.min, cNH, Op.add)
            for a in range(8):
                for h in range(2):
                    mm(("S", CM + a, CM + 8 * ne, 8), blk("BA", a), ("V2", 8 * h, 8 * h + ne), group=("cm", t, a))
        for c, o0, w, how in chs:
            i = INST.index((t, c))
            A = w // 16
            kd, ks = split(t, c)
            VL, gr = (vl(t, c), 0, w), ("vl", i)
            for k in range(15, -1, -1) if c >= 2 and VL[0] in ("VL0", "VL1") else ():
                mm(VL, ("YB", 15 - k, 143 - k), ("C", cat[c, k], cat[c, k] + w), group=gr)
            at = {}
            if natural(t, c):
                q0 = take("QS", 16 * w)
                for v0 in range(0, w, 128):
                    if v0 >= w - cfg["NV"]:
                        for h in range(v0, v0 + 128, 32):
                            cp(("QS", q0 + 16 * h, q0 + 16 * h + 512), ("ind", (W, 0, top), ("OT1", h, h + 32)))
                        continue
                    j = act(("QS", q0 + 16 * v0, q0 + 16 * v0 + 2048), ("ind", (W, 0, top), ("OT1", v0, v0 + 128)), Fn.Copy)
                    ops[j]["soft"] = prevq[-1:]
                    prevq.append(j)
                for k in range(16):
                    mm(VL, blk("ND", k), ("QS", q0 + k, q0 + 16 * w, 16), group=gr)
                kd = ks = 0
            for k0, k1 in kcalls(0, ks, cfg["KQ"]):
                q0 = take("QS", (k1 - k0) * w)
                j = act(("QS", q0, q0 + (k1 - k0) * w), ("ind", (W, 0, top), (OT, o0 + k0 * A, o0 + k1 * A)), Fn.Copy)
                ops[j]["soft"] = prevq[-1:]
                prevq.append(j)
                for k in range(k0, k1):
                    at[k] = ("QS", q0 + (k - k0) * w, q0 + (k - k0 + 1) * w)
                    if k < kd:
                        j = dma("S", ("QD", o0, o0 + w), at[k], "dq%d" % i, group=("dq", i), rows=k)
                        ops[j]["lat"] += cfg["dp0"] if c == 0 else 0.0
                    else:
                        mm(VL, blk("ND", k), at[k], group=gr)
            for k0, k1 in kcalls(ks, 16, cfg["KW"]) if not natural(t, c) else ():
                q0 = take("QH", (k1 - k0) * w)
                cp(("QH", q0, q0 + (k1 - k0) * w), ("ind", (W, 0, top), (OT, o0 + k0 * A, o0 + k1 * A)))
                for k in range(k0, k1):
                    mm(VL, blk("NH", k - 8), ("QH", q0 + (k - k0) * w, q0 + (k - k0 + 1) * w), group=gr)
            if kd:
                mm(VL, blk("NI", kds.index(kd)), ("QD", o0, o0 + w), group=gr)
            EN = ("T3", o0, o0 + w)
            tt(EN, (W, G + o0, G + o0 + w), VL, Op.min)
            act((WN, G + o0, G + o0 + w), EN, Fn.Abs)
            while todo and todo[0][1] + todo[0][2] <= min(o0 + w, L0):
                ch = todo.pop(0)
                offsets(t + 1, WN, ch[1], ch[2], VL[0], True)
        LA = ("LA", 0, 128)
        scale("l", LA, ("ind", (WN, G, NP), MO), col("NR", 4 + t))
        tt(("ind", (WN, G, NP), MO), LA, ("CH", 0, 128), Op.add)
        if last:
            dma("S", ("yn", 0, L0), (WN, G, G + L0), "st3")
        tt(("ind", (WN, G + L0, NP), CO) if t else (WN, G + L0, G + L0 + CAP), LA, ("GG", 0, 128), Op.add)
        for j, ch in enumerate(todo):
            offsets(t + 1, WN, ch[1], ch[2], "VL%d" % ((i + j) % 2))
        if last:
            dma("A", ("yn", L0, LM), (WN, G + L0, NP), "st2")
    return ops


def schedule(ops, cfg=CFG):
    if cfg.get("sets"):
        return arrange2(cfg)
    if cfg.get("turns"):
        return arrange(ops, cfg)
    n = len(ops)
    succ = [[] for _ in range(n)]
    for o in ops:
        for d in o["deps"]:
            succ[d].append(o["id"])

    def span(o):
        return o["cost"] + (o["lat"] + o["busy"] if "busy" in o else 0.0)

    prio = [0.0] * n
    for o in reversed(ops):
        prio[o["id"]] = max(prio[o["id"]], span(o) + cfg["sem"] + max([prio[s] for s in succ[o["id"]]], default=0.0))
        for j in o.get("soft", ()) if "CH" in cfg else ():
            prio[j] = max(prio[j], prio[o["id"]] + ops[j]["cost"])
    left = [len(o["deps"]) for o in ops]
    ready_at = [0.0] * n
    done = [0.0] * n
    start = [0.0] * n
    pool = {e: [] for e in "VAPGSX"}
    free = {e: 0.0 for e in "VAPGS"}
    state = {"dma": 0.0, "first": True}
    order = {e: [] for e in "VAPGS"}
    issued = set()

    def release(i):
        for s in succ[i]:
            ready_at[s] = max(ready_at[s], done[i] + cfg["sem"])
            left[s] -= 1
            if left[s] == 0:
                if ops[s]["eng"] == "X":
                    start[s] = ready_at[s]
                    done[s] = ready_at[s] + ops[s]["cost"]
                    release(s)
                else:
                    pool[ops[s]["eng"]].append(s)

    for o in ops:
        if not o["deps"]:
            pool[o["eng"]].append(o["id"])
    while True:
        best = None
        for e in "VAPGS":
            can = [i for i in pool[e] if all(j in issued for j in ops[i].get("soft", ()))]
            if can:
                tm = max(free[e], min(ready_at[i] for i in can))
                if best is None or tm < best[0]:
                    best = (tm, e, can)
        if best is None:
            break
        tm, e, can = best
        i = max((i for i in can if ready_at[i] <= tm + cfg["look"]), key=lambda j: (prio[j], -j))
        tm = max(tm, ready_at[i])
        pool[e].remove(i)
        issued.add(i)
        o = ops[i]
        start[i] = tm
        free[e] = tm + o["cost"]
        if "busy" in o:
            extra = 0.0
            if e == "G" and state["first"]:
                state["first"] = False
                extra = cfg["first"]
            s0 = max(free[e] + o["lat"] / 2 + extra, state["dma"])
            state["dma"] = s0 + o["busy"]
            done[i] = state["dma"] + o["lat"] / 2
        else:
            done[i] = free[e]
        order[e].append(i)
        release(i)
    return order, start, done


lam = [1e9]


def sweep(nodes, before, after, prio, look):
    n = len(nodes)
    left = [len(b) for b in before]
    ready = [0.0] * n
    start = [0.0] * n
    pool = {e: [] for e in "VAPGSD"}
    free = {e: 0.0 for e in pool}
    order = {e: [] for e in pool}
    todo = [i for i in range(n) if not left[i]]

    def settle():
        while todo:
            i = todo.pop()
            if nodes[i][0] == "X":
                finish(i, ready[i])
            else:
                pool[nodes[i][0]].append(i)

    def finish(i, tm):
        start[i] = tm
        for s, delay in after[i]:
            ready[s] = max(ready[s], tm + nodes[i][1] + delay)
            left[s] -= 1
            if not left[s]:
                todo.append(s)

    settle()
    while True:
        best = None
        for e in pool:
            if pool[e]:
                tm = max(free[e], min(ready[i] for i in pool[e]))
                if best is None or tm < best[0]:
                    best = (tm, e)
        if best is None:
            return order, start
        tm, e = best
        if e == "D" and look is not None:
            i = min(pool[e], key=lambda j: ready[j])
        else:
            i = max((i for i in pool[e] if ready[i] <= tm), key=lambda j: (prio[j], -j))
            soon = [j for j in pool[e] if tm < ready[j] < tm + nodes[i][1] and prio[j] > prio[i]]
            if soon and look != 0.0:
                j = max(soon, key=lambda j: prio[j])
                wait = ready[j] - tm
                if max(wait + prio[j], wait + nodes[j][1] + prio[i]) + abs(look or lam[0]) * wait < max(prio[i], nodes[i][1] + prio[j]):
                    i = j
        tm = max(tm, ready[i])
        pool[e].remove(i)
        free[e] = tm + nodes[i][1]
        order[e].append(i)
        finish(i, tm)
        settle()


def arrange(ops, cfg=CFG):
    n = len(ops)
    nodes = [(o["eng"], o["cost"]) for o in ops]
    tail = {}
    edges = []
    first = True
    for o in ops:
        if "busy" in o:
            tail[o["id"]] = len(nodes)
            nodes.append(("D", o["busy"]))
            edges.append((o["id"], tail[o["id"]], o["lat"] / 2 + (cfg["first"] if first and o["eng"] == "G" else 0.0)))
            first = first and o["eng"] != "G"
    for o in ops:
        for d in o["deps"]:
            if d in tail:
                edges.append((tail[d], o["id"], ops[d]["lat"] / 2 + cfg["sem"]))
            else:
                edges.append((d, o["id"], cfg["sem"]))
        for d in o.get("soft", ()):
            edges.append((d, o["id"], 0.0))
    m = len(nodes)
    before, after = [[] for _ in range(m)], [[] for _ in range(m)]
    for a, b, delay in edges:
        after[a].append((b, delay))
        before[b].append((a, delay))
    prio = [-float(i) for i in range(n)] + [0.0] * (m - n)
    best = None
    for turn in range(cfg["turns"]):
        order, start = sweep(nodes, before, after, prio, cfg["look"])
        done = [start[i] + nodes[i][1] for i in range(m)]
        if best is None or max(done) < best[0] or cfg["keep"]:
            best = (max(done), order, start, done)
        if "all" in cfg:
            cfg["all"].append({e: order[e] for e in "VAPGS"})
        back = sweep(nodes, after, before, done, None)[1]
        prio = [back[i] + nodes[i][1] for i in range(m)]
    end, order, start, done = best
    for i in tail:
        done[i] = done[tail[i]] + ops[i]["lat"] / 2
    return {e: order[e] for e in "VAPGS"}, start[:n], done[:n]


def sweep2(eng, cost, before, after, prio, look, fifo):
    n, k = cost.shape
    left = [len(b) for b in before]
    ready = np.zeros((n, k))
    start = np.zeros((n, k))
    mean = [0.0] * n
    pool = {e: [] for e in "VAPGSD"}
    free = {e: np.zeros(k) for e in pool}
    fmean = {e: 0.0 for e in pool}
    order = {e: [] for e in pool}
    todo = [i for i in range(n) if not left[i]]

    def finish(i, tm):
        start[i] = tm
        end = tm + cost[i]
        for s, delay in after[i]:
            np.maximum(ready[s], end + delay, out=ready[s])
            left[s] -= 1
            if not left[s]:
                todo.append(s)

    def settle():
        while todo:
            i = todo.pop()
            if eng[i] == "X":
                finish(i, ready[i])
            else:
                mean[i] = float(ready[i].mean())
                pool[eng[i]].append(i)

    settle()
    while True:
        best = None
        for e in pool:
            if pool[e]:
                tm = max(fmean[e], min(mean[i] for i in pool[e]))
                if best is None or tm < best[0]:
                    best = (tm, e)
        if best is None:
            return order, start
        tm, e = best
        can = pool[e]
        if len(can) == 1:
            i = can[0]
        elif e == "D" and fifo:
            i = min(can, key=lambda j: mean[j])
        else:
            wait = np.maximum(ready[can] - free[e], 0.0).mean(axis=1)
            i = max(zip(can, wait), key=lambda x: (prio[x[0]] - look * x[1], -x[0]))[0]
        tm = np.maximum(free[e], ready[i])
        can.remove(i)
        free[e] = tm + cost[i]
        fmean[e] = float(free[e].mean())
        order[e].append(i)
        finish(i, tm)
        settle()


def arrange2(cfg=CFG):
    sets = [dict(cfg, **s) for s in cfg["sets"]]
    built = [build(s) for s in sets]
    ops = built[0]
    n = len(ops)
    unit = np.array([1.0 / max(sum(o["cost"] for o in b if o["eng"] == e) for e in "VA") for b in built]) * 180000.0
    eng = [o["eng"] for o in ops]
    cost = [[b[i]["cost"] for b in built] for i in range(n)]
    sem = np.array([s["sem"] for s in sets]) * unit
    tail, lat, edges, first = {}, {}, [], True
    for o in ops:
        if "busy" in o:
            i = o["id"]
            tail[i] = len(eng)
            eng.append("D")
            cost.append([b[i]["busy"] for b in built])
            lat[i] = np.array([b[i]["lat"] / 2 for b in built]) * unit
            extra = np.array([s["first"] for s in sets]) * unit if first and o["eng"] == "G" else 0.0
            edges.append((i, tail[i], lat[i] + extra))
            first = first and o["eng"] != "G"
    for o in ops:
        for d in o["deps"]:
            edges.append((tail[d], o["id"], lat[d] + sem) if d in tail else (d, o["id"], sem))
        for d in o.get("soft", ()):
            edges.append((d, o["id"], 0.0))
    cost = np.array(cost) * unit
    m = len(eng)
    before, after = [[] for _ in range(m)], [[] for _ in range(m)]
    for a, b, delay in edges:
        after[a].append((b, delay))
        before[b].append((a, delay))
    prio = [-float(i) for i in range(n)] + [0.0] * (m - n)
    best = None
    for turn in range(cfg["turns"]):
        order, start = sweep2(eng, cost, before, after, prio, cfg["look"], True)
        done = start + cost
        ends = done.max(axis=0)
        mark = float(ends.mean() + 0.5 * ends.max())
        if best is None or mark < best[0]:
            best = (mark, order, start.mean(axis=1), done.mean(axis=1))
        back = sweep2(eng, cost, after, before, list(done.mean(axis=1)), cfg["look"], False)[1]
        prio = list((back + cost).mean(axis=1))
    mark, order, start, done = best
    return {e: order[e] for e in "VAPGS"}, list(start[:n]), list(done[:n])


PLAN = []


def plan():
    if not PLAN:
        ops = build()
        order, start, done = schedule(ops)
        PLAN.append((ops, order, start, done))
    return PLAN[0]


def helper_program(g, core, owner, T, topo):
    rid, pid, _ = topo.addr(owner)
    m = topo.mask(core, owner)
    sent = 0
    for o in plan()[0]:
        if o["kind"] == "fold":
            i, o0, w = o["args"]
            g.wait_ge(T.sem["ha%d" % i], 16)
            g.remote_dma(T.Y[:, o0:o0 + w], T.Y[:, o0:o0 + w], T.sem["ya%d" % i], T.sem.hback, pid, rid, m)
            sent += len(topo.engines(core, owner))
    g.wait_ge(T.sem.hback, sent)


def rank_program(g, core, T, topo):
    rank = T.rank_of(core)
    if rank is None:
        for c in T.cores:
            if helper_of(c, T, topo) == core:
                helper_program(g, core, c, T, topo)
        return
    ops, order, start, done = plan()
    queue = {"V": g.vector, "A": g.scalar, "P": g.tensor, "G": g, "S": g.sync}
    helper = helper_of(core, T, topo)

    def ap(a):
        if not isinstance(a, tuple):
            return a
        if a[0] == "ind":
            return ap(a[1]).indirect(ap(a[2]))
        if len(a) > 3:
            return T[a[0]][:, a[1]:a[2]:a[3]]
        return T[a[0]][:, a[1]:a[2]]

    total = {}
    for o in ops:
        if "sem" in o:
            total[o["sem"]] = total.get(o["sem"], 0) + o["inc"]
    needed = set()
    for o in ops:
        needed |= o["deps"]
    event = {}
    for o in ops:
        if "sem" in o:
            event[o["id"]] = (o["sem"], total[o["sem"]])
    for e in "VAPG":
        k = 0
        for i in order[e]:
            if i not in event and i in needed:
                k += 1
                event[i] = (ESEM[e], k)
        total[ESEM[e]] = k
    first, lastin = {}, {}
    for i in order["P"]:
        gr = ops[i]["group"]
        if gr is not None:
            first.setdefault(gr, i)
            lastin[gr] = i

    def issue(q, o):
        kind, a = o["kind"], o["args"]
        if kind == "mm":
            gr = o["group"]
            return q.matmul(ap(a[0]), ap(a[1]), ap(a[2]), gr is None or first[gr] == o["id"], gr is None or lastin[gr] == o["id"])
        if kind == "iota":
            if SCRATCH[a[0][0]][2] == "int32":
                return q.iota(ap(a[0]), a[1], a[2], a[3])
            return q.iota(ap(a[0]), a[1], a[2], a[3], allow_small_or_imprecise_dtypes=True)
        if kind == "select":
            return q.affine_select(ap(a[0]), ap(a[1]), *a[2:])
        if kind == "dma":
            if a[2] is None:
                return q.dma_start(ap(a[0]), ap(a[1]))
            return q.dma_start(T[a[0][0]][a[2]::16, a[0][1]:a[0][2]], T[a[1][0]][a[2]::16, a[1][1]:a[1][2]])
        if kind == "send":
            buf, t = a
            trs = []
            for d in range(2):
                dst = T.cores[(rank - OFF[d]) % N]
                rid, pid, _ = topo.addr(dst)
                en = topo.engines(core, dst)
                half = en[d * len(en) // 2:(d + 1) * len(en) // 2]
                trs.append(RemoteDMATransfer(dst_ids=[DstId(rid=rid, pnc=pid)], dma_engine_mask=mask_of(half),
                                             remote_sem=T.sem[("ga%d", "gb%d")[d] % t], src=T[buf][:, G:G + B], dst=T[buf][:, d * B:d * B + B]))
            g.remote_dma_fused(trs, local_sem=T.sem[o["sem"]])
            return None
        if kind == "fold":
            i, o0, w = a
            rid, pid, _ = topo.addr(helper)
            tr = RemoteDMATransfer(dst_ids=[DstId(rid=rid, pnc=pid)], dma_engine_mask=topo.mask(core, helper), remote_sem=T.sem["ha%d" % i],
                                   srcs=[T.P[:, 16 * o0 + k * w:16 * o0 + k * w + w] for k in range(16)], dsts=[T.Y[:, o0:o0 + w]], alu_op=2)
            g.remote_dma_fused([tr], local_sem=T.sem[o["sem"]])
            return None
        out, ins, x = a
        if kind == "ts":
            if x[1] is None:
                return q.tensor_scalar(ap(out), ap(ins[0]), ap(ins[1]), None, x[0])
            return q.tensor_scalar(ap(out), ap(ins[0]), ap(ins[1]), ap(ins[2]), x[0], x[1])
        if kind == "tt":
            return q.tensor_tensor(ap(out), ap(ins[0]), ap(ins[1]), x)
        if kind == "cp":
            return q.tensor_copy(ap(out), ap(ins[0]))
        if kind == "tr":
            return q.transpose(ap(out), ap(ins[0]))
        if kind == "scan":
            return q.tensor_tensor_scan(ap(out), ap(ins[0]), ap(ins[1]), ap(ins[2]), Op.mult, Op.add)
        if ins[1] is not None:
            return q.activation(ap(out), ap(ins[0]), x, bias=ap(ins[1]), scale=ap(ins[2]))
        if ins[2] is None:
            return q.activation(ap(out), ap(ins[0]), x)
        return q.activation(ap(out), ap(ins[0]), x, scale=ap(ins[2]))

    for e in "SAVPG":
        q = queue[e]
        known = {}
        for i in order[e]:
            o = ops[i]
            want = {}
            for d in o["deps"]:
                if d in event:
                    s, v = event[d]
                    want[s] = max(want.get(s, 0), v)
            for s, v in sorted(want.items()):
                if known.get(s, 0) < v:
                    q.wait_ge(T.sem[s], v)
                    known[s] = v
            ins = issue(q, o)
            if ins is not None and i in event:
                ins.then_inc(T.sem[event[i][0]], 16 if "sem" in o else 1)
        if e == "G":
            for s, v in sorted(total.items()):
                if v and known.get(s, 0) < v:
                    q.wait_ge(T.sem[s], v)
